import numpy as np
import ml_dtypes


def mxq(x, axis, fmt="e4m3"):
    dtype, down = {"e4m3": (ml_dtypes.float8_e4m3fn, 7), "e5m2": (ml_dtypes.float8_e5m2, 14)}[fmt]
    v = np.moveaxis(np.asarray(x, np.float32).astype(ml_dtypes.bfloat16).astype(np.float64), axis, -1)
    blocks = v.reshape(v.shape[:-1] + (-1, 32))
    amax = np.abs(blocks).max(-1, keepdims=True)
    byte = np.maximum(np.where(amax > 0, np.frexp(amax)[1] - 1 + 127, 0) - down, 1)
    scale = np.exp2(byte - 127.0)
    codes = (blocks / scale).astype(np.float32).astype(dtype).astype(np.float64)
    return np.moveaxis((codes * scale).reshape(v.shape), -1, axis)


WIDE = False


def mx_kscale(k):
    if not WIDE:
        return np.ones(k)
    levels = np.array([10, -10, 5, -5, 0])
    if k % 512:
        return np.exp2(np.random.permutation(np.resize(levels, k // 32))).repeat(32)
    a = np.empty((k // 512, 16))
    for p in range(k // 512):
        a[p, :8] = np.random.permutation(np.resize(levels, 8))
        for g in range(8):
            far = levels[np.abs(levels - a[p, g]) >= 10]
            a[p, g + 8] = far[np.random.randint(len(far))]
    return np.exp2(a.ravel()).repeat(32)


def f64(x):
    return np.asarray(x).astype(np.float64)


def striped(idx):
    return np.tile(idx.reshape(-1, 16).T, (8, 1)).astype(np.uint16)


def unstriped(offs):
    return offs[:16].T.reshape(-1).astype(np.int64)


E2M1 = np.array([0.0, 0.5, 1.0, 1.5, 2.0, 3.0, 4.0, 6.0, -0.0, -0.5, -1.0, -1.5, -2.0, -3.0, -4.0, -6.0])


def pack_weight(w, fmt):
    k, n = w.shape
    w = f64(np.asarray(w, np.float32).astype(ml_dtypes.bfloat16)).reshape(k // 32, 32, n)
    amax = np.abs(w).max(1)
    if fmt == "e4m3":
        byte = np.frexp(amax)[1] - 1 + 127 - 7
    else:
        mant, ex = np.frexp(amax / 6.0)
        byte = np.where(mant > 0.5, ex, ex - 1) + 127
    byte = np.clip(np.where(amax > 0, byte, 1), 1, 254)
    scaled = (w * np.exp2(127.0 - byte)[:, None, :]).reshape(k, n).astype(np.float32)
    by_word = np.ascontiguousarray(scaled.reshape(k // 512, 128, 4, n).transpose(0, 1, 3, 2))
    if fmt == "e4m3":
        words = by_word.astype(ml_dtypes.float8_e4m3fn).view(np.uint8)
    else:
        c = by_word.astype(ml_dtypes.float4_e2m1fn).view(np.uint8) & 0xF
        words = (c[..., 0::2] | (c[..., 1::2] << 4)).reshape(k // 512, 128, 2 * n)
    return np.ascontiguousarray(words), np.ascontiguousarray(byte.astype(np.uint8).reshape(k // 512, 16, n))


def unpack_weight(words, scales, fmt):
    g, _, n = scales.shape
    words = np.ascontiguousarray(words).reshape(g, 128, n, -1)
    if fmt == "e4m3":
        vals = words.view(ml_dtypes.float8_e4m3fn).astype(np.float64)
    else:
        nib = np.empty((g, 128, n, 4), np.uint8)
        nib[..., 0::2] = words & 0xF
        nib[..., 1::2] = words >> 4
        vals = E2M1[nib]
    vals = vals * np.repeat(np.exp2(scales.astype(np.float64) - 127.0), 8, axis=1)[..., None]
    return vals.transpose(0, 1, 3, 2).reshape(g * 512, n)


def gelu(v):
    return 0.5 * v * (1.0 + np.tanh(np.sqrt(2.0 / np.pi) * (v + 0.044715 * v**3)))


def silu(v):
    return v / (1.0 + np.exp(-np.maximum(v, -700.0)))


K, T, E, C, H, N = 512, 768, 6, 128, 512, 128


def by_expert(wq, xq):
    return np.concatenate([wq[e].T @ xq[:, e * C:(e + 1) * C] for e in range(E)], axis=1)


def setup_inputs():
    n = np.random.standard_normal
    s = mx_kscale(K)
    u = mx_kscale(H)
    slot_token = np.random.permutation(T)[:E * C]
    x = pack_weight(n((K, T)) * s[:, None], "e4m3")
    wg = pack_weight(n((K, N)) / np.sqrt(K) / s[:, None], "e4m3")
    w1 = [pack_weight(m, "e2m1") for m in n((E, K, H)) / np.sqrt(K) / s[None, :, None] * u]
    w2 = [pack_weight(m, "e2m1") for m in n((E, H, N)) / np.sqrt(H) / u[None, :, None]]
    return {
        "x_words": x[0],
        "x_scales": x[1],
        "wg_words": wg[0],
        "wg_scales": wg[1],
        "w1_words": np.stack([m[0] for m in w1]),
        "w1_scales": np.stack([m[1] for m in w1]),
        "w2_words": np.stack([m[0] for m in w2]),
        "w2_scales": np.stack([m[1] for m in w2]),
        "gate": np.tile(np.random.uniform(0.2, 1.0, E * C), (128, 1)).astype(np.float32),
        "offs": striped(slot_token),
    }


def reference(x_words, x_scales, wg_words, wg_scales, w1_words, w1_scales, w2_words, w2_scales, gate, offs):
    wg = unpack_weight(wg_words, wg_scales, "e4m3")
    w1 = np.stack([unpack_weight(w1_words[e], w1_scales[e], "e2m1") for e in range(E)])
    w2 = np.stack([unpack_weight(w2_words[e], w2_scales[e], "e2m1") for e in range(E)])
    idx = unstriped(offs)
    x = unpack_weight(x_words, x_scales, "e4m3")
    o = silu(wg.T @ x)
    h = gelu(by_expert(w1, x[:, idx]))
    y = by_expert(w2, mxq(h, 0, "e4m3"))
    c = np.zeros((N, T))
    c[:, idx] = f64(gate[:1]) * y
    return o * c

@@ -1,0 +1,189 @@
+from contextlib import ExitStack
+
+import concourse.mybir as mybir
+from concourse.masks import make_identity
+
+K, T, E, C, H, N = 512, 768, 6, 128, 512, 128
+FLOPS = 2 * K * N * T + 2 * K * H * E * C + 2 * H * N * E * C
+
+F32 = mybir.dt.float32
+BF16 = mybir.dt.bfloat16
+I32 = mybir.dt.int32
+U32 = mybir.dt.uint32
+U16 = mybir.dt.uint16
+U8 = mybir.dt.uint8
+FP8X4 = mybir.dt.float8_e4m3fn_x4
+FP4X4 = mybir.dt.float4_e2m1fn_x4
+ACT = mybir.ActivationFunctionType
+MULT = mybir.AluOpType.mult
+
+P = 128
+LIST_COLS = C // 16
+GATHER_GROUPS = ((0,), (1,), (2, 3), (4, 5))
+BACK_GROUPS = ((0,), (1,), (2, 3), (4,), (5,))
+COPY_ON_VECTOR = (False, False, False, False, True)
+GATE_COLS = ((0, 512), (512, 768))
+OUT_COLS = ((0, 256), (256, 512), (512, 768))
+
+
+def tile_moe_ogt_gelu_silu_kernel(
+    tc, x_words, x_scales, wg_words, wg_scales, w1_words, w1_scales, w2_words, w2_scales, gate, offs, out
+):
+    nc = tc.nc
+    with ExitStack() as ctx:
+        keep = ctx.enter_context(tc.tile_pool(name="keep", bufs=1))
+        psum_h = ctx.enter_context(tc.psum_pool(name="psum_h", bufs=3))
+        psum_t = ctx.enter_context(tc.psum_pool(name="psum_t", bufs=2))
+        psum_y = ctx.enter_context(tc.psum_pool(name="psum_y", bufs=3))
+
+        offsets = keep.tile([P, E * LIST_COLS], U16, name="offsets")
+        xw = keep.tile([P, T], I32, name="xw", align_bytes=64)
+        xs = keep.tile([P, T], U8, name="xs", align_bytes=64)
+        w1s = keep.tile([P, E, H], U8, name="w1s", align_bytes=64)
+        w2s = keep.tile([P, E, N], U8, name="w2s", align_bytes=64)
+        wgs = keep.tile([P, N], U8, name="wgs", align_bytes=64)
+        w1 = keep.tile([P, E, 2 * H], U8, name="w1", align_bytes=64)
+        w2 = keep.tile([P, E, 2 * N], U8, name="w2", align_bytes=64)
+        wg = keep.tile([P, N], I32, name="wg", align_bytes=64)
+        gates = keep.tile([P, E * C], F32, name="gates", align_bytes=64)
+        ident = keep.tile([P, P], F32, name="ident", align_bytes=64)
+        warm = keep.tile([P, 8], F32, name="warm", align_bytes=64)
+
+        nc.vector.memset(xs[:].bitcast(I32), 0)
+        nc.vector.memset(warm[:, 0:1], 0.0)
+        nc.vector.memset(w1s[:].bitcast(I32), 0)
+        nc.vector.memset(w2s[:].bitcast(I32), 0)
+        nc.vector.memset(wgs[:].bitcast(I32), 0)
+        nc.scalar.activation(warm[:, 1:2], warm[:, 0:1], ACT.Gelu_apprx_tanh)
+
+        def load_plane(plane, rows, queues=(nc.sync,) * 4):
+            for q in range(4):
+                queues[q].dma_start(out=plane[32 * q : 32 * q + 4].bitcast(I32), in_=rows[4 * q : 4 * q + 4].bitcast(I32))
+
+        nc.sync.dma_start(offsets[:], offs)
+        nc.sync.dma_start(out=xw[:], in_=x_words[0].rearrange("p t d -> p (t d)").bitcast(I32))
+
+        def load_w1(queue, lo, hi):
+            queue.dma_start(
+                out=w1[:, lo:hi, :].bitcast(I32), in_=w1_words[lo:hi, 0].rearrange("e p b -> p e b").bitcast(I32)
+            )
+
+        load_w1(nc.gpsimd, 0, 1)
+        load_plane(xs, x_scales[0])
+        load_plane(w1s, w1_scales[:, 0].rearrange("e r n -> r e n"), (nc.gpsimd, nc.sync, nc.sync, nc.sync))
+        make_identity(nc, ident[:])
+        load_w1(nc.sync, 1, 3)
+        load_w1(nc.sync, 3, 6)
+        load_plane(w2s, w2_scales[:, 0].rearrange("e r n -> r e n"))
+        nc.sync.dma_start(out=w2[:].bitcast(I32), in_=w2_words[:, 0].rearrange("e p b -> p e b").bitcast(I32))
+        nc.sync.dma_start(out=gates[:], in_=gate)
+        load_plane(wgs, wg_scales[0])
+        nc.sync.dma_start(out=wg[:], in_=wg_words[0].rearrange("p n d -> p (n d)").bitcast(I32))
+
+        def list_of(grp):
+            return offsets[:, grp[0] * LIST_COLS : (grp[-1] + 1) * LIST_COLS]
+
+        gathered = {}
+        for grp in GATHER_GROUPS:
+            gw = keep.tile([P, len(grp) * C], U32, name=f"gw{grp[0]}", align_bytes=64)
+            gs = keep.tile([P, len(grp) * C], U8, name=f"gs{grp[0]}", align_bytes=64)
+            nc.vector.tensor_copy(gw[:], xw[:].bitcast(U32).indirect(list_of(grp)))
+            nc.vector.tensor_copy(gs[:], xs[:].indirect(list_of(grp)))
+            for u, e in enumerate(grp):
+                gathered[e] = (gw[:, u * C : (u + 1) * C], gs[:, u * C : (u + 1) * C])
+
+        combined = keep.tile([P, T], F32, name="combined", align_bytes=64)
+
+        hidden = {}
+
+        def first_layer(e):
+            words, scales = gathered[e]
+            pre = psum_h.tile([P, H], F32, name="pre")
+            nc.tensor.matmul_mx(
+                out=pre[:], lhsT=words.bitcast(FP8X4), lhsT_scale=scales,
+                rhs=w1[:, e, :].bitcast(FP4X4), rhs_scale=w1s[:, e, :], start=True, stop=True,
+            )
+            hb = keep.tile([P, H], BF16, name=f"hb{e}", align_bytes=64)
+            nc.scalar.activation(
+                hb[:].rearrange("s (u p d) -> s u p d", u=2, d=2),
+                pre[:].rearrange("s (p u d) -> s u p d", u=2, d=2),
+                ACT.Gelu_apprx_tanh,
+            )
+            hidden[e] = hb
+
+        def turn(gi):
+            grp = BACK_GROUPS[gi]
+            n = len(grp)
+            turned = psum_t.tile([P, 4 * C], F32, name="turned")
+            for u, e in enumerate(grp):
+                pairs = hidden[e][:].bitcast(F32)
+                for half in range(2):
+                    col = (2 * u + half) * C
+                    nc.tensor.transpose(turned[:, col : col + C], pairs[:, half * P : (half + 1) * P], ident[:])
+            ht = keep.tile([P, n * C * 4], BF16, name=f"ht{gi}", align_bytes=64)
+            dst = ht[:].bitcast(F32).rearrange("p (e s u) -> p e s u", e=n, u=2)
+            src = turned[:, : 2 * n * C].rearrange("p (e u s) -> p e s u", e=n, u=2)
+            if COPY_ON_VECTOR[gi]:
+                nc.vector.tensor_copy(dst, src)
+            else:
+                nc.scalar.copy(dst, src)
+            return ht
+
+        def second_layer(gi, ht):
+            grp = BACK_GROUPS[gi]
+            n = len(grp)
+            hq = keep.tile([P, n * C], U32, name=f"hq{gi}", align_bytes=64)
+            hs = keep.tile([P, n * C], U8, name=f"hs{gi}", align_bytes=64)
+            nc.vector.quantize_mx(out=hq[:].bitcast(FP8X4), scales=hs[:], in_=ht[:])
+            y = psum_y.tile([P, 2 * C], F32, name="y")
+            for u, e in enumerate(grp):
+                cols = slice(u * C, (u + 1) * C)
+                nc.tensor.matmul_mx(
+                    out=y[:, cols], lhsT=w2[:, e, :].bitcast(FP4X4), lhsT_scale=w2s[:, e, :],
+                    rhs=hq[:, cols].bitcast(FP8X4), rhs_scale=hs[:, cols], start=True, stop=True,
+                )
+            return y
+
+        def go_back(gi, y):
+            grp = BACK_GROUPS[gi]
+            n = len(grp)
+            weighted = keep.tile([P, n * C], F32, name=f"weighted{gi}", align_bytes=64)
+            nc.vector.tensor_tensor(weighted[:], y[:, : n * C], gates[:, grp[0] * C : (grp[-1] + 1) * C], MULT)
+            nc.vector.tensor_copy(combined[:].indirect(list_of(grp)), weighted[:])
+
+        first_layer(0)
+        first_layer(1)
+        ht0 = turn(0)
+        first_layer(2)
+        ht1 = turn(1)
+        first_layer(3)
+        y0 = second_layer(0, ht0)
+        y1 = second_layer(1, ht1)
+        first_layer(4)
+        ht2 = turn(2)
+        go_back(0, y0)
+        first_layer(5)
+        go_back(1, y1)
+        y2 = second_layer(2, ht2)
+        ht3 = turn(3)
+        ht4 = turn(4)
+        y3 = second_layer(3, ht3)
+        go_back(2, y2)
+        y4 = second_layer(4, ht4)
+
+        opened = keep.tile([P, T], F32, name="opened", align_bytes=64)
+        for lo, hi in GATE_COLS:
+            pre_gate = psum_t.tile([P, 4 * C], F32, name="turned")
+            nc.tensor.matmul_mx(
+                out=pre_gate[:, : hi - lo], lhsT=wg[:].bitcast(FP8X4), lhsT_scale=wgs[:],
+                rhs=xw[:, lo:hi].bitcast(FP8X4), rhs_scale=xs[:, lo:hi], start=True, stop=True,
+            )
+            nc.scalar.activation(opened[:, lo:hi], pre_gate[:, : hi - lo], ACT.Silu)
+
+        go_back(3, y3)
+        go_back(4, y4)
+
+        result = keep.tile([P, T], F32, name="result", align_bytes=64)
+        for lo, hi in OUT_COLS:
+            nc.vector.tensor_tensor(result[:, lo:hi], combined[:, lo:hi], opened[:, lo:hi], MULT)
+            nc.sync.dma_start(out=out[:, lo:hi], in_=result[:, lo:hi])

@@ -21,7 +21,8 @@ P = 128
 LIST_COLS = C // 16
 GATHER_GROUPS = ((0,), (1,), (2, 3), (4, 5))
 BACK_GROUPS = ((0,), (1,), (2, 3), (4,), (5,))
-COPY_ON_VECTOR = (False, False, False, False, True)
+SCATTER_GROUPS = ((0,), (1,), (2, 3), (4, 5))
+COPY_ON_VECTOR = (False, False, False, False, False)
 GATE_COLS = ((0, 512), (512, 768))
 OUT_COLS = ((0, 256), (256, 512), (512, 768))
 
@@ -43,18 +44,19 @@ def tile_moe_ogt_gelu_silu_kernel(
         w2s = keep.tile([P, E, N], U8, name="w2s", align_bytes=64)
         wgs = keep.tile([P, N], U8, name="wgs", align_bytes=64)
         w1 = keep.tile([P, E, 2 * H], U8, name="w1", align_bytes=64)
-        w2 = keep.tile([P, E, 2 * N], U8, name="w2", align_bytes=64)
         wg = keep.tile([P, N], I32, name="wg", align_bytes=64)
-        gates = keep.tile([P, E * C], F32, name="gates", align_bytes=64)
         ident = keep.tile([P, P], F32, name="ident", align_bytes=64)
-        warm = keep.tile([P, 8], F32, name="warm", align_bytes=64)
+        warm_in = keep.tile([P, 1], F32, name="warm_in", tag="late_a", align_bytes=64)
+        warm_out = keep.tile([P, 1], F32, name="warm_out", tag="late_b", align_bytes=64)
 
         nc.vector.memset(xs[:].bitcast(I32), 0)
-        nc.vector.memset(warm[:, 0:1], 0.0)
+        nc.vector.memset(warm_in[:], 0.0)
         nc.vector.memset(w1s[:].bitcast(I32), 0)
         nc.vector.memset(w2s[:].bitcast(I32), 0)
         nc.vector.memset(wgs[:].bitcast(I32), 0)
-        nc.scalar.activation(warm[:, 1:2], warm[:, 0:1], ACT.Gelu_apprx_tanh)
+        nc.scalar.activation(warm_out[:], warm_in[:], ACT.Gelu_apprx_tanh)
+        w2 = keep.tile([P, E, 2 * N], U8, name="w2", tag="late_a", align_bytes=64)
+        gates = keep.tile([P, E * C], F32, name="gates", tag="late_b", align_bytes=64)
 
         def load_plane(plane, rows, queues=(nc.sync,) * 4):
             for q in range(4):
@@ -68,17 +70,16 @@ def tile_moe_ogt_gelu_silu_kernel(
                 out=w1[:, lo:hi, :].bitcast(I32), in_=w1_words[lo:hi, 0].rearrange("e p b -> p e b").bitcast(I32)
             )
 
-        load_w1(nc.gpsimd, 0, 1)
-        load_plane(xs, x_scales[0])
-        load_plane(w1s, w1_scales[:, 0].rearrange("e r n -> r e n"), (nc.gpsimd, nc.sync, nc.sync, nc.sync))
         make_identity(nc, ident[:])
-        load_w1(nc.sync, 1, 3)
-        load_w1(nc.sync, 3, 6)
+        load_w1(nc.gpsimd, 0, 3)
+        load_w1(nc.gpsimd, 3, 6)
+        load_plane(xs, x_scales[0])
+        load_plane(w1s, w1_scales[:, 0].rearrange("e r n -> r e n"))
         load_plane(w2s, w2_scales[:, 0].rearrange("e r n -> r e n"))
         nc.sync.dma_start(out=w2[:].bitcast(I32), in_=w2_words[:, 0].rearrange("e p b -> p e b").bitcast(I32))
         nc.sync.dma_start(out=gates[:], in_=gate)
         load_plane(wgs, wg_scales[0])
-        nc.sync.dma_start(out=wg[:], in_=wg_words[0].rearrange("p n d -> p (n d)").bitcast(I32))
+        nc.gpsimd.dma_start(out=wg[:], in_=wg_words[0].rearrange("p n d -> p (n d)").bitcast(I32))
 
         def list_of(grp):
             return offsets[:, grp[0] * LIST_COLS : (grp[-1] + 1) * LIST_COLS]
@@ -129,23 +130,24 @@ def tile_moe_ogt_gelu_silu_kernel(
                 nc.scalar.copy(dst, src)
             return ht
 
-        def second_layer(gi, ht):
+        def second_layer(gi, ht, y=None, first=0):
             grp = BACK_GROUPS[gi]
             n = len(grp)
             hq = keep.tile([P, n * C], U32, name=f"hq{gi}", align_bytes=64)
             hs = keep.tile([P, n * C], U8, name=f"hs{gi}", align_bytes=64)
             nc.vector.quantize_mx(out=hq[:].bitcast(FP8X4), scales=hs[:], in_=ht[:])
-            y = psum_y.tile([P, 2 * C], F32, name="y")
+            if y is None:
+                y = psum_y.tile([P, 2 * C], F32, name="y")
             for u, e in enumerate(grp):
                 cols = slice(u * C, (u + 1) * C)
                 nc.tensor.matmul_mx(
-                    out=y[:, cols], lhsT=w2[:, e, :].bitcast(FP4X4), lhsT_scale=w2s[:, e, :],
+                    out=y[:, first + u * C : first + (u + 1) * C], lhsT=w2[:, e, :].bitcast(FP4X4), lhsT_scale=w2s[:, e, :],
                     rhs=hq[:, cols].bitcast(FP8X4), rhs_scale=hs[:, cols], start=True, stop=True,
                 )
             return y
 
         def go_back(gi, y):
-            grp = BACK_GROUPS[gi]
+            grp = SCATTER_GROUPS[gi]
             n = len(grp)
             weighted = keep.tile([P, n * C], F32, name=f"weighted{gi}", align_bytes=64)
             nc.vector.tensor_tensor(weighted[:], y[:, : n * C], gates[:, grp[0] * C : (grp[-1] + 1) * C], MULT)
@@ -169,7 +171,7 @@ def tile_moe_ogt_gelu_silu_kernel(
         ht4 = turn(4)
         y3 = second_layer(3, ht3)
         go_back(2, y2)
-        y4 = second_layer(4, ht4)
+        second_layer(4, ht4, y3, C)
 
         opened = keep.tile([P, T], F32, name="opened", align_bytes=64)
         for lo, hi in GATE_COLS:
@@ -181,7 +183,6 @@ def tile_moe_ogt_gelu_silu_kernel(
             nc.scalar.activation(opened[:, lo:hi], pre_gate[:, : hi - lo], ACT.Silu)
 
         go_back(3, y3)
-        go_back(4, y4)
 
         result = keep.tile([P, T], F32, name="result", align_bytes=64)
         for lo, hi in OUT_COLS:

@@ -1,7 +1,6 @@
 from contextlib import ExitStack
 
 import concourse.mybir as mybir
-from concourse.masks import make_identity
 
 K, T, E, C, H, N = 512, 768, 6, 128, 512, 128
 FLOPS = 2 * K * N * T + 2 * K * H * E * C + 2 * H * N * E * C
@@ -16,13 +15,14 @@ FP8X4 = mybir.dt.float8_e4m3fn_x4
 FP4X4 = mybir.dt.float4_e2m1fn_x4
 ACT = mybir.ActivationFunctionType
 MULT = mybir.AluOpType.mult
+ADD = mybir.AluOpType.add
 
 P = 128
 LIST_COLS = C // 16
-GATHER_GROUPS = ((0,), (1,), (2, 3), (4, 5))
-BACK_GROUPS = ((0,), (1,), (2, 3), (4,), (5,))
-SCATTER_GROUPS = ((0,), (1,), (2, 3), (4, 5))
-COPY_ON_VECTOR = (False, False, False, False, False)
+PRE_BANK = "ABCBEF"
+TURN_BANK = "DEFADC"
+SUM_BANK = "CBEFA"
+GATE_BANK = "FC"
 GATE_COLS = ((0, 512), (512, 768))
 OUT_COLS = ((0, 256), (256, 512), (512, 768))
 
@@ -33,9 +33,10 @@ def tile_moe_ogt_gelu_silu_kernel(
     nc = tc.nc
     with ExitStack() as ctx:
         keep = ctx.enter_context(tc.tile_pool(name="keep", bufs=1))
-        psum_h = ctx.enter_context(tc.psum_pool(name="psum_h", bufs=3))
-        psum_t = ctx.enter_context(tc.psum_pool(name="psum_t", bufs=2))
-        psum_y = ctx.enter_context(tc.psum_pool(name="psum_y", bufs=3))
+        psum = ctx.enter_context(tc.psum_pool(name="psum", bufs=1))
+
+        def bank(tag):
+            return psum.tile([P, 512], F32, name=tag, tag=tag)
 
         offsets = keep.tile([P, E * LIST_COLS], U16, name="offsets")
         xw = keep.tile([P, T], I32, name="xw", align_bytes=64)
@@ -43,146 +44,183 @@ def tile_moe_ogt_gelu_silu_kernel(
         w1s = keep.tile([P, E, H], U8, name="w1s", align_bytes=64)
         w2s = keep.tile([P, E, N], U8, name="w2s", align_bytes=64)
         wgs = keep.tile([P, N], U8, name="wgs", align_bytes=64)
-        w1 = keep.tile([P, E, 2 * H], U8, name="w1", align_bytes=64)
+        w1a = keep.tile([P, 2, 2 * H], U8, name="w1a", align_bytes=64)
+        w1b = keep.tile([P, 4, 2 * H], U8, name="w1b", align_bytes=64)
         wg = keep.tile([P, N], I32, name="wg", align_bytes=64)
         ident = keep.tile([P, P], F32, name="ident", align_bytes=64)
-        warm_in = keep.tile([P, 1], F32, name="warm_in", tag="late_a", align_bytes=64)
-        warm_out = keep.tile([P, 1], F32, name="warm_out", tag="late_b", align_bytes=64)
+        warm_in = keep.tile([P, 1], F32, name="warm_in", align_bytes=64)
+        warm_out = keep.tile([P, 1], F32, name="warm_out", align_bytes=64)
 
-        nc.vector.memset(xs[:].bitcast(I32), 0)
-        nc.vector.memset(warm_in[:], 0.0)
+        ones = keep.tile([P, 32], F32, name="ones", align_bytes=64)
         nc.vector.memset(w1s[:].bitcast(I32), 0)
+        nc.vector.memset(warm_in[:], 0.0)
+        nc.vector.memset(ones[:], 1.0)
         nc.vector.memset(w2s[:].bitcast(I32), 0)
         nc.vector.memset(wgs[:].bitcast(I32), 0)
-        nc.scalar.activation(warm_out[:], warm_in[:], ACT.Gelu_apprx_tanh)
-        w2 = keep.tile([P, E, 2 * N], U8, name="w2", tag="late_a", align_bytes=64)
-        gates = keep.tile([P, E * C], F32, name="gates", tag="late_b", align_bytes=64)
+        w2 = keep.tile([P, E, 2 * N], U8, name="w2", align_bytes=64)
+        gates = keep.tile([P, E * C], F32, name="gates", align_bytes=64)
 
-        def load_plane(plane, rows, queues=(nc.sync,) * 4):
+        def load_plane(plane, rows):
             for q in range(4):
-                queues[q].dma_start(out=plane[32 * q : 32 * q + 4].bitcast(I32), in_=rows[4 * q : 4 * q + 4].bitcast(I32))
+                nc.sync.dma_start(out=plane[32 * q : 32 * q + 4].bitcast(I32), in_=rows[4 * q : 4 * q + 4].bitcast(I32))
+
+        def load_w1(tile, lo, hi):
+            nc.gpsimd.dma_start(
+                out=tile[:].bitcast(I32), in_=w1_words[lo:hi, 0].rearrange("e p b -> p e b").bitcast(I32)
+            )
 
         nc.sync.dma_start(offsets[:], offs)
         nc.sync.dma_start(out=xw[:], in_=x_words[0].rearrange("p t d -> p (t d)").bitcast(I32))
-
-        def load_w1(queue, lo, hi):
-            queue.dma_start(
-                out=w1[:, lo:hi, :].bitcast(I32), in_=w1_words[lo:hi, 0].rearrange("e p b -> p e b").bitcast(I32)
-            )
-
-        make_identity(nc, ident[:])
-        load_w1(nc.gpsimd, 0, 3)
-        load_w1(nc.gpsimd, 3, 6)
-        load_plane(xs, x_scales[0])
-        load_plane(w1s, w1_scales[:, 0].rearrange("e r n -> r e n"))
-        load_plane(w2s, w2_scales[:, 0].rearrange("e r n -> r e n"))
-        nc.sync.dma_start(out=w2[:].bitcast(I32), in_=w2_words[:, 0].rearrange("e p b -> p e b").bitcast(I32))
-        nc.sync.dma_start(out=gates[:], in_=gate)
-        load_plane(wgs, wg_scales[0])
+        x_rows = x_scales[0].bitcast(I32)
+        nc.scalar.dma_start(out=xs[0:98].bitcast(I32), in_=x_rows[0:14].unsqueeze(0).to_broadcast([7, 14, T // 4]))
+        nc.sync.dma_start(out=xs[98:128].bitcast(I32), in_=x_rows[14:16].unsqueeze(0).to_broadcast([15, 2, T // 4]))
+        load_w1(w1a, 0, 2)
+        load_w1(w1b, 2, 6)
+        nc.gpsimd.dma_start(out=w2[:].bitcast(I32), in_=w2_words[:, 0].rearrange("e p b -> p e b").bitcast(I32))
+        nc.gpsimd.dma_start(out=gates[:], in_=gate)
         nc.gpsimd.dma_start(out=wg[:], in_=wg_words[0].rearrange("p n d -> p (n d)").bitcast(I32))
+        load_plane(w1s, w1_scales[:, 0].rearrange("e r n -> r e n"))
+        nc.scalar.activation(warm_out[:], warm_in[:], ACT.Gelu_apprx_tanh)
+        load_plane(w2s, w2_scales[:, 0].rearrange("e r n -> r e n"))
+        load_plane(wgs, wg_scales[0])
 
-        def list_of(grp):
-            return offsets[:, grp[0] * LIST_COLS : (grp[-1] + 1) * LIST_COLS]
+        ramp = keep.tile([P, 32], F32, name="ramp", align_bytes=64)
+        lane = keep.tile([P, 32], F32, name="lane", align_bytes=64)
+        nc.vector.memset(ident[:], 0.0)
+        nc.vector.tensor_tensor_scan(ramp[:], ones[:], ones[:], 0.0, MULT, ADD)
+        nc.vector.transpose(lane[:], ramp[:])
+        for q in range(4):
+            part = slice(32 * q, 32 * q + 32)
+            nc.vector.tensor_tensor(ident[part, part], ramp[part, :], lane[part, :], mybir.AluOpType.is_equal)
 
-        gathered = {}
-        for grp in GATHER_GROUPS:
-            gw = keep.tile([P, len(grp) * C], U32, name=f"gw{grp[0]}", align_bytes=64)
-            gs = keep.tile([P, len(grp) * C], U8, name=f"gs{grp[0]}", align_bytes=64)
-            nc.vector.tensor_copy(gw[:], xw[:].bitcast(U32).indirect(list_of(grp)))
-            nc.vector.tensor_copy(gs[:], xs[:].indirect(list_of(grp)))
-            for u, e in enumerate(grp):
-                gathered[e] = (gw[:, u * C : (u + 1) * C], gs[:, u * C : (u + 1) * C])
+        def list_of(lo, hi):
+            return offsets[:, lo * LIST_COLS : hi * LIST_COLS]
+
+        words, scales, codes, banks = {}, {}, {}, {}
+
+        def gather_scales(lo, hi, tag):
+            gs = keep.tile([P, (hi - lo) * C], U8, name=f"gs{lo}", tag=tag, align_bytes=64)
+            nc.vector.tensor_copy(gs[:], xs[:].indirect(list_of(lo, hi)))
+            for e in range(lo, hi):
+                scales[e] = gs[:, (e - lo) * C : (e - lo + 1) * C]
+
+        def gather_words(lo, hi, tag):
+            gw = keep.tile([P, (hi - lo) * C], U32, name=f"gw{lo}", tag=tag, align_bytes=64)
+            nc.vector.tensor_copy(gw[:], xw[:].bitcast(U32).indirect(list_of(lo, hi)))
+            for e in range(lo, hi):
+                words[e] = gw[:, (e - lo) * C : (e - lo + 1) * C]
 
         combined = keep.tile([P, T], F32, name="combined", align_bytes=64)
+        pre, hidden, turned, ready, sums, plain = {}, {}, {}, {}, {}, {}
 
-        hidden = {}
-
-        def first_layer(e):
-            words, scales = gathered[e]
-            pre = psum_h.tile([P, H], F32, name="pre")
+        def first_product(e):
+            pre[e] = bank(PRE_BANK[e])
+            w1 = w1a[:, e, :] if e < 2 else w1b[:, e - 2, :]
             nc.tensor.matmul_mx(
-                out=pre[:], lhsT=words.bitcast(FP8X4), lhsT_scale=scales,
-                rhs=w1[:, e, :].bitcast(FP4X4), rhs_scale=w1s[:, e, :], start=True, stop=True,
+                out=pre[e][:], lhsT=words[e].bitcast(FP8X4), lhsT_scale=scales[e],
+                rhs=w1.bitcast(FP4X4), rhs_scale=w1s[:, e, :], start=True, stop=True,
             )
+
+        def gelu(e):
             hb = keep.tile([P, H], BF16, name=f"hb{e}", align_bytes=64)
             nc.scalar.activation(
                 hb[:].rearrange("s (u p d) -> s u p d", u=2, d=2),
-                pre[:].rearrange("s (p u d) -> s u p d", u=2, d=2),
+                pre[e][:].rearrange("s (p u d) -> s u p d", u=2, d=2),
                 ACT.Gelu_apprx_tanh,
             )
             hidden[e] = hb
 
-        def turn(gi):
-            grp = BACK_GROUPS[gi]
-            n = len(grp)
-            turned = psum_t.tile([P, 4 * C], F32, name="turned")
-            for u, e in enumerate(grp):
-                pairs = hidden[e][:].bitcast(F32)
-                for half in range(2):
-                    col = (2 * u + half) * C
-                    nc.tensor.transpose(turned[:, col : col + C], pairs[:, half * P : (half + 1) * P], ident[:])
-            ht = keep.tile([P, n * C * 4], BF16, name=f"ht{gi}", align_bytes=64)
-            dst = ht[:].bitcast(F32).rearrange("p (e s u) -> p e s u", e=n, u=2)
-            src = turned[:, : 2 * n * C].rearrange("p (e u s) -> p e s u", e=n, u=2)
-            if COPY_ON_VECTOR[gi]:
-                nc.vector.tensor_copy(dst, src)
+        def turn(e):
+            turned[e] = bank(TURN_BANK[e])
+            pairs = hidden[e][:].bitcast(F32)
+            for half in range(2):
+                nc.tensor.transpose(turned[e][:, half * C : (half + 1) * C], pairs[:, half * P : (half + 1) * P], ident[:])
+
+        def interleave(e):
+            ht = keep.tile([P, C * 4], BF16, name=f"ht{e}", align_bytes=64)
+            nc.scalar.copy(
+                ht[:].bitcast(F32).rearrange("p (s u) -> p s u", u=2),
+                turned[e][:, : 2 * C].rearrange("p (u s) -> p s u", u=2),
+            )
+            ready[e] = ht
+
+        def quantise(e):
+            hq = keep.tile([P, C], U32, name=f"hq{e}", align_bytes=64)
+            hs = keep.tile([P, C], U8, name=f"hs{e}", align_bytes=64)
+            nc.vector.quantize_mx(out=hq[:].bitcast(FP8X4), scales=hs[:], in_=ready[e][:])
+            codes[e] = (hq, hs)
+
+        def second_product(e):
+            hq, hs = codes[e]
+            if e < 5:
+                banks[e] = bank(SUM_BANK[e])
+                sums[e] = banks[e][:, :C]
             else:
-                nc.scalar.copy(dst, src)
-            return ht
+                sums[e] = banks[4][:, C : 2 * C]
+            nc.tensor.matmul_mx(
+                out=sums[e], lhsT=w2[:, e, :].bitcast(FP4X4), lhsT_scale=w2s[:, e, :],
+                rhs=hq[:].bitcast(FP8X4), rhs_scale=hs[:], start=True, stop=True,
+            )
 
-        def second_layer(gi, ht, y=None, first=0):
-            grp = BACK_GROUPS[gi]
-            n = len(grp)
-            hq = keep.tile([P, n * C], U32, name=f"hq{gi}", align_bytes=64)
-            hs = keep.tile([P, n * C], U8, name=f"hs{gi}", align_bytes=64)
-            nc.vector.quantize_mx(out=hq[:].bitcast(FP8X4), scales=hs[:], in_=ht[:])
-            if y is None:
-                y = psum_y.tile([P, 2 * C], F32, name="y")
-            for u, e in enumerate(grp):
-                cols = slice(u * C, (u + 1) * C)
-                nc.tensor.matmul_mx(
-                    out=y[:, first + u * C : first + (u + 1) * C], lhsT=w2[:, e, :].bitcast(FP4X4), lhsT_scale=w2s[:, e, :],
-                    rhs=hq[:, cols].bitcast(FP8X4), rhs_scale=hs[:, cols], start=True, stop=True,
-                )
-            return y
+        for lo, hi in ((0, 1), (1, 2), (2, 4), (4, 6)):
+            plain[lo] = keep.tile([P, (hi - lo) * C], F32, name=f"plain{lo}", align_bytes=64)
 
-        def go_back(gi, y):
-            grp = SCATTER_GROUPS[gi]
-            n = len(grp)
-            weighted = keep.tile([P, n * C], F32, name=f"weighted{gi}", align_bytes=64)
-            nc.vector.tensor_tensor(weighted[:], y[:, : n * C], gates[:, grp[0] * C : (grp[-1] + 1) * C], MULT)
-            nc.vector.tensor_copy(combined[:].indirect(list_of(grp)), weighted[:])
+        def unload(e):
+            lo = min(e, 2)
+            nc.scalar.copy(plain[lo][:, (e - lo) * C : (e - lo + 1) * C], sums[e])
 
-        first_layer(0)
-        first_layer(1)
-        ht0 = turn(0)
-        first_layer(2)
-        ht1 = turn(1)
-        first_layer(3)
-        y0 = second_layer(0, ht0)
-        y1 = second_layer(1, ht1)
-        first_layer(4)
-        ht2 = turn(2)
-        go_back(0, y0)
-        first_layer(5)
-        go_back(1, y1)
-        y2 = second_layer(2, ht2)
-        ht3 = turn(3)
-        ht4 = turn(4)
-        y3 = second_layer(3, ht3)
-        go_back(2, y2)
-        second_layer(4, ht4, y3, C)
+        def scatter_gated(lo, hi):
+            nc.vector.tensor_tensor(
+                combined[:].indirect(list_of(lo, hi)), plain[lo][:], gates[:, lo * C : hi * C], MULT
+            )
+
+        gather_words(0, 1, "words0")
+        gather_words(1, 2, "words1")
+        for e in range(3):
+            gather_scales(e, e + 1, f"scales{e}")
+        gather_scales(3, 6, "scales3")
+        first_product(0)
+        gather_words(2, 3, "words0")
+        first_product(1)
+        gather_words(3, 6, "words1")
+        first_product(2)
+        gelu(0)
+        turn(0)
+        gelu(1)
+        turn(1)
+        first_product(3)
+        interleave(0)
+        quantise(0)
+        for e in range(1, 5):
+            gelu(e + 1)
+            turn(e + 1)
+            second_product(e - 1)
+            interleave(e)
+            if e + 3 < E:
+                first_product(e + 3)
+            quantise(e)
+            if e > 1:
+                unload(e - 2)
+            if e in (2, 3):
+                scatter_gated(e - 2, e - 1)
+        second_product(4)
+        interleave(5)
+        quantise(5)
+        second_product(5)
+        unload(3)
+        scatter_gated(2, 4)
 
         opened = keep.tile([P, T], F32, name="opened", align_bytes=64)
-        for lo, hi in GATE_COLS:
-            pre_gate = psum_t.tile([P, 4 * C], F32, name="turned")
+        for (lo, hi), tag in zip(GATE_COLS, GATE_BANK):
+            pre_gate = bank(tag)
             nc.tensor.matmul_mx(
                 out=pre_gate[:, : hi - lo], lhsT=wg[:].bitcast(FP8X4), lhsT_scale=wgs[:],
                 rhs=xw[:, lo:hi].bitcast(FP8X4), rhs_scale=xs[:, lo:hi], start=True, stop=True,
             )
             nc.scalar.activation(opened[:, lo:hi], pre_gate[:, : hi - lo], ACT.Silu)
 
-        go_back(3, y3)
+        nc.vector.tensor_tensor(plain[4][:], banks[4][:, : 2 * C], gates[:, 4 * C :], MULT)
+        nc.vector.tensor_copy(combined[:].indirect(list_of(4, 6)), plain[4][:])
 
         result = keep.tile([P, T], F32, name="result", align_bytes=64)
         for lo, hi in OUT_COLS:

@@ -48,50 +48,51 @@ def tile_moe_ogt_gelu_silu_kernel(
         w1b = keep.tile([P, 4, 2 * H], U8, name="w1b", align_bytes=64)
         wg = keep.tile([P, N], I32, name="wg", align_bytes=64)
         ident = keep.tile([P, P], F32, name="ident", align_bytes=64)
-        warm_in = keep.tile([P, 1], F32, name="warm_in", align_bytes=64)
         warm_out = keep.tile([P, 1], F32, name="warm_out", align_bytes=64)
-
         ones = keep.tile([P, 32], F32, name="ones", align_bytes=64)
-        nc.vector.memset(w1s[:].bitcast(I32), 0)
-        nc.vector.memset(warm_in[:], 0.0)
-        nc.vector.memset(ones[:], 1.0)
-        nc.vector.memset(w2s[:].bitcast(I32), 0)
-        nc.vector.memset(wgs[:].bitcast(I32), 0)
-        w2 = keep.tile([P, E, 2 * N], U8, name="w2", align_bytes=64)
-        gates = keep.tile([P, E * C], F32, name="gates", align_bytes=64)
+        ramp = keep.tile([P, 32], F32, name="ramp", align_bytes=64)
+        lane = keep.tile([P, 32], F32, name="lane", align_bytes=64)
 
-        def load_plane(plane, rows):
+        def load_plane(plane, rows, queues):
             for q in range(4):
-                nc.sync.dma_start(out=plane[32 * q : 32 * q + 4].bitcast(I32), in_=rows[4 * q : 4 * q + 4].bitcast(I32))
+                queues[q].dma_start(
+                    out=plane[32 * q : 32 * q + 4].bitcast(I32), in_=rows[4 * q : 4 * q + 4].bitcast(I32)
+                )
 
-        def load_w1(tile, lo, hi):
-            nc.gpsimd.dma_start(
+        def load_w1(queue, tile, lo, hi):
+            queue.dma_start(
                 out=tile[:].bitcast(I32), in_=w1_words[lo:hi, 0].rearrange("e p b -> p e b").bitcast(I32)
             )
 
+        sync, scalar = nc.sync, nc.scalar
+        nc.vector.memset(w1s[:].bitcast(I32), 0)
+        nc.vector.memset(ones[:], 1.0)
         nc.sync.dma_start(offsets[:], offs)
         nc.sync.dma_start(out=xw[:], in_=x_words[0].rearrange("p t d -> p (t d)").bitcast(I32))
         x_rows = x_scales[0].bitcast(I32)
         nc.scalar.dma_start(out=xs[0:98].bitcast(I32), in_=x_rows[0:14].unsqueeze(0).to_broadcast([7, 14, T // 4]))
         nc.sync.dma_start(out=xs[98:128].bitcast(I32), in_=x_rows[14:16].unsqueeze(0).to_broadcast([15, 2, T // 4]))
-        load_w1(w1a, 0, 2)
-        load_w1(w1b, 2, 6)
-        nc.gpsimd.dma_start(out=w2[:].bitcast(I32), in_=w2_words[:, 0].rearrange("e p b -> p e b").bitcast(I32))
-        nc.gpsimd.dma_start(out=gates[:], in_=gate)
-        nc.gpsimd.dma_start(out=wg[:], in_=wg_words[0].rearrange("p n d -> p (n d)").bitcast(I32))
-        load_plane(w1s, w1_scales[:, 0].rearrange("e r n -> r e n"))
-        nc.scalar.activation(warm_out[:], warm_in[:], ACT.Gelu_apprx_tanh)
-        load_plane(w2s, w2_scales[:, 0].rearrange("e r n -> r e n"))
-        load_plane(wgs, wg_scales[0])
+        load_w1(nc.gpsimd, w1a, 0, 2)
+        load_plane(w1s, w1_scales[:, 0].rearrange("e r n -> r e n"), (scalar, scalar, sync, scalar))
+        load_w1(nc.sync, w1b, 2, 6)
 
-        ramp = keep.tile([P, 32], F32, name="ramp", align_bytes=64)
-        lane = keep.tile([P, 32], F32, name="lane", align_bytes=64)
-        nc.vector.memset(ident[:], 0.0)
         nc.vector.tensor_tensor_scan(ramp[:], ones[:], ones[:], 0.0, MULT, ADD)
+        nc.scalar.activation(warm_out[:], ramp[:, 0:1], ACT.Gelu_apprx_tanh, bias=ones[:, 0:1])
+        nc.vector.memset(ident[:], 0.0)
         nc.vector.transpose(lane[:], ramp[:])
         for q in range(4):
             part = slice(32 * q, 32 * q + 32)
             nc.vector.tensor_tensor(ident[part, part], ramp[part, :], lane[part, :], mybir.AluOpType.is_equal)
+
+        nc.vector.memset(w2s[:].bitcast(I32), 0)
+        nc.vector.memset(wgs[:].bitcast(I32), 0)
+        w2 = keep.tile([P, E, 2 * N], U8, name="w2", tag="warm_out", align_bytes=64)
+        gates = keep.tile([P, E * C], F32, name="gates", tag="ones", align_bytes=64)
+        load_plane(w2s, w2_scales[:, 0].rearrange("e r n -> r e n"), (sync,) * 4)
+        nc.scalar.dma_start(out=w2[:].bitcast(I32), in_=w2_words[:, 0].rearrange("e p b -> p e b").bitcast(I32))
+        nc.scalar.dma_start(out=gates[:], in_=gate)
+        load_plane(wgs, wg_scales[0], (sync,) * 4)
+        nc.sync.dma_start(out=wg[:], in_=wg_words[0].rearrange("p n d -> p (n d)").bitcast(I32))
 
         def list_of(lo, hi):
             return offsets[:, lo * LIST_COLS : hi * LIST_COLS]

@@ -22,8 +22,8 @@ LIST_COLS = C // 16
 PRE_BANK = "ABCBEF"
 TURN_BANK = "DEFADC"
 SUM_BANK = "CBEFA"
-GATE_BANK = "FC"
-GATE_COLS = ((0, 512), (512, 768))
+GATE_BANK = "GH"
+GATE_COLS = ((0, 256), (256, 768))
 OUT_COLS = ((0, 256), (256, 512), (512, 768))
 
 
@@ -45,7 +45,8 @@ def tile_moe_ogt_gelu_silu_kernel(
         w2s = keep.tile([P, E, N], U8, name="w2s", align_bytes=64)
         wgs = keep.tile([P, N], U8, name="wgs", align_bytes=64)
         w1a = keep.tile([P, 2, 2 * H], U8, name="w1a", align_bytes=64)
-        w1b = keep.tile([P, 4, 2 * H], U8, name="w1b", align_bytes=64)
+        w1b = keep.tile([P, 2, 2 * H], U8, name="w1b", align_bytes=64)
+        w1c = keep.tile([P, 2, 2 * H], U8, name="w1c", align_bytes=64)
         wg = keep.tile([P, N], I32, name="wg", align_bytes=64)
         ident = keep.tile([P, P], F32, name="ident", align_bytes=64)
         warm_out = keep.tile([P, 1], F32, name="warm_out", align_bytes=64)
@@ -65,16 +66,18 @@ def tile_moe_ogt_gelu_silu_kernel(
             )
 
         sync, scalar = nc.sync, nc.scalar
+        nc.vector.memset(xs[:].bitcast(I32), 0)
         nc.vector.memset(w1s[:].bitcast(I32), 0)
         nc.vector.memset(ones[:], 1.0)
         nc.sync.dma_start(offsets[:], offs)
         nc.sync.dma_start(out=xw[:], in_=x_words[0].rearrange("p t d -> p (t d)").bitcast(I32))
         x_rows = x_scales[0].bitcast(I32)
         nc.scalar.dma_start(out=xs[0:98].bitcast(I32), in_=x_rows[0:14].unsqueeze(0).to_broadcast([7, 14, T // 4]))
-        nc.sync.dma_start(out=xs[98:128].bitcast(I32), in_=x_rows[14:16].unsqueeze(0).to_broadcast([15, 2, T // 4]))
-        load_w1(nc.gpsimd, w1a, 0, 2)
+        nc.sync.dma_start(out=xs[98:100].bitcast(I32), in_=x_rows[14:16])
+        load_w1(nc.sync, w1a, 0, 2)
         load_plane(w1s, w1_scales[:, 0].rearrange("e r n -> r e n"), (scalar, scalar, sync, scalar))
-        load_w1(nc.sync, w1b, 2, 6)
+        load_w1(nc.sync, w1b, 2, 4)
+        load_w1(nc.sync, w1c, 4, 6)
 
         nc.vector.tensor_tensor_scan(ramp[:], ones[:], ones[:], 0.0, MULT, ADD)
         nc.scalar.activation(warm_out[:], ramp[:, 0:1], ACT.Gelu_apprx_tanh, bias=ones[:, 0:1])
@@ -116,7 +119,7 @@ def tile_moe_ogt_gelu_silu_kernel(
 
         def first_product(e):
             pre[e] = bank(PRE_BANK[e])
-            w1 = w1a[:, e, :] if e < 2 else w1b[:, e - 2, :]
+            w1 = (w1a, w1b, w1c)[e // 2][:, e % 2, :]
             nc.tensor.matmul_mx(
                 out=pre[e][:], lhsT=words[e].bitcast(FP8X4), lhsT_scale=scales[e],
                 rhs=w1.bitcast(FP4X4), rhs_scale=w1s[:, e, :], start=True, stop=True,
@@ -211,19 +214,21 @@ def tile_moe_ogt_gelu_silu_kernel(
         unload(3)
         scatter_gated(2, 4)
 
-        opened = keep.tile([P, T], F32, name="opened", align_bytes=64)
+        pre_gate = []
         for (lo, hi), tag in zip(GATE_COLS, GATE_BANK):
-            pre_gate = bank(tag)
+            pre_gate.append(bank(tag))
             nc.tensor.matmul_mx(
-                out=pre_gate[:, : hi - lo], lhsT=wg[:].bitcast(FP8X4), lhsT_scale=wgs[:],
+                out=pre_gate[-1][:, : hi - lo], lhsT=wg[:].bitcast(FP8X4), lhsT_scale=wgs[:],
                 rhs=xw[:, lo:hi].bitcast(FP8X4), rhs_scale=xs[:, lo:hi], start=True, stop=True,
             )
-            nc.scalar.activation(opened[:, lo:hi], pre_gate[:, : hi - lo], ACT.Silu)
-
-        nc.vector.tensor_tensor(plain[4][:], banks[4][:, : 2 * C], gates[:, 4 * C :], MULT)
-        nc.vector.tensor_copy(combined[:].indirect(list_of(4, 6)), plain[4][:])
+        opened_a = keep.tile([P, 256], F32, name="opened_a", tag="ht5", align_bytes=64)
+        opened_b = keep.tile([P, 512], F32, name="opened_b", tag="hq5", align_bytes=64)
+        nc.scalar.activation(opened_a[:], pre_gate[0][:, :256], ACT.Silu)
+        nc.scalar.copy(plain[4][:], banks[4][:, : 2 * C])
+        nc.scalar.activation(opened_b[:], pre_gate[1][:], ACT.Silu)
+        scatter_gated(4, 6)
 
         result = keep.tile([P, T], F32, name="result", align_bytes=64)
-        for lo, hi in OUT_COLS:
-            nc.vector.tensor_tensor(result[:, lo:hi], combined[:, lo:hi], opened[:, lo:hi], MULT)
+        for (lo, hi), opened in zip(OUT_COLS, (opened_a[:], opened_b[:, :256], opened_b[:, 256:])):
+            nc.vector.tensor_tensor(result[:, lo:hi], combined[:, lo:hi], opened, MULT)
             nc.sync.dma_start(out=out[:, lo:hi], in_=result[:, lo:hi])

@@ -19,10 +19,10 @@ ADD = mybir.AluOpType.add
 
 P = 128
 LIST_COLS = C // 16
-PRE_BANK = "ABCBEF"
-TURN_BANK = "DEFADC"
-SUM_BANK = "CBEFA"
-GATE_BANK = "GH"
+PRE_BANK = "ABCABC"
+TURN_BANK = "DEFGDE"
+SUM_BANK = "GHFFAA"
+GATE_BANK = "BC"
 GATE_COLS = ((0, 256), (256, 768))
 OUT_COLS = ((0, 256), (256, 512), (512, 768))
 
@@ -42,7 +42,6 @@ def tile_moe_ogt_gelu_silu_kernel(
         xw = keep.tile([P, T], I32, name="xw", align_bytes=64)
         xs = keep.tile([P, T], U8, name="xs", align_bytes=64)
         w1s = keep.tile([P, E, H], U8, name="w1s", align_bytes=64)
-        w2s = keep.tile([P, E, N], U8, name="w2s", align_bytes=64)
         wgs = keep.tile([P, N], U8, name="wgs", align_bytes=64)
         w1a = keep.tile([P, 2, 2 * H], U8, name="w1a", align_bytes=64)
         w1b = keep.tile([P, 2, 2 * H], U8, name="w1b", align_bytes=64)
@@ -72,10 +71,10 @@ def tile_moe_ogt_gelu_silu_kernel(
         nc.sync.dma_start(offsets[:], offs)
         nc.sync.dma_start(out=xw[:], in_=x_words[0].rearrange("p t d -> p (t d)").bitcast(I32))
         x_rows = x_scales[0].bitcast(I32)
+        nc.scalar.dma_start(out=xs[98:100].bitcast(I32), in_=x_rows[14:16])
         nc.scalar.dma_start(out=xs[0:98].bitcast(I32), in_=x_rows[0:14].unsqueeze(0).to_broadcast([7, 14, T // 4]))
-        nc.sync.dma_start(out=xs[98:100].bitcast(I32), in_=x_rows[14:16])
         load_w1(nc.sync, w1a, 0, 2)
-        load_plane(w1s, w1_scales[:, 0].rearrange("e r n -> r e n"), (scalar, scalar, sync, scalar))
+        load_plane(w1s, w1_scales[:, 0].rearrange("e r n -> r e n"), (scalar, sync, scalar, sync))
         load_w1(nc.sync, w1b, 2, 4)
         load_w1(nc.sync, w1c, 4, 6)
 
@@ -87,13 +86,12 @@ def tile_moe_ogt_gelu_silu_kernel(
             part = slice(32 * q, 32 * q + 32)
             nc.vector.tensor_tensor(ident[part, part], ramp[part, :], lane[part, :], mybir.AluOpType.is_equal)
 
+        w2s = keep.tile([P, E, N], U8, name="w2s", align_bytes=64)
         nc.vector.memset(w2s[:].bitcast(I32), 0)
         nc.vector.memset(wgs[:].bitcast(I32), 0)
-        w2 = keep.tile([P, E, 2 * N], U8, name="w2", tag="warm_out", align_bytes=64)
-        gates = keep.tile([P, E * C], F32, name="gates", tag="ones", align_bytes=64)
-        load_plane(w2s, w2_scales[:, 0].rearrange("e r n -> r e n"), (sync,) * 4)
-        nc.scalar.dma_start(out=w2[:].bitcast(I32), in_=w2_words[:, 0].rearrange("e p b -> p e b").bitcast(I32))
-        nc.scalar.dma_start(out=gates[:], in_=gate)
+        w2 = keep.tile([P, E, 2 * N], U8, name="w2", align_bytes=64)
+        load_plane(w2s, w2_scales[:, 0].rearrange("e r n -> r e n"), (scalar, sync, scalar, sync))
+        nc.sync.dma_start(out=w2[:].bitcast(I32), in_=w2_words[:, 0].rearrange("e p b -> p e b").bitcast(I32))
         load_plane(wgs, wg_scales[0], (sync,) * 4)
         nc.sync.dma_start(out=wg[:], in_=wg_words[0].rearrange("p n d -> p (n d)").bitcast(I32))
 
@@ -116,6 +114,10 @@ def tile_moe_ogt_gelu_silu_kernel(
 
         combined = keep.tile([P, T], F32, name="combined", align_bytes=64)
         pre, hidden, turned, ready, sums, plain = {}, {}, {}, {}, {}, {}
+        pair = {}
+        hb_tag = {5: "hs0"}
+        hq_tag = {0: "hb1", 1: "hb2"}
+
 
         def first_product(e):
             pre[e] = bank(PRE_BANK[e])
@@ -126,7 +128,7 @@ def tile_moe_ogt_gelu_silu_kernel(
             )
 
         def gelu(e):
-            hb = keep.tile([P, H], BF16, name=f"hb{e}", align_bytes=64)
+            hb = keep.tile([P, H], BF16, name=f"hb{e}", tag=hb_tag.get(e, f"hb{e}"), align_bytes=64)
             nc.scalar.activation(
                 hb[:].rearrange("s (u p d) -> s u p d", u=2, d=2),
                 pre[e][:].rearrange("s (p u d) -> s u p d", u=2, d=2),
@@ -141,78 +143,99 @@ def tile_moe_ogt_gelu_silu_kernel(
                 nc.tensor.transpose(turned[e][:, half * C : (half + 1) * C], pairs[:, half * P : (half + 1) * P], ident[:])
 
         def interleave(e):
-            ht = keep.tile([P, C * 4], BF16, name=f"ht{e}", align_bytes=64)
-            nc.scalar.copy(
+            if e == 5:
+                ht = pair["ht"][:, C * 4 :]
+            elif e == 4:
+                pair["ht"] = keep.tile([P, C * 8], BF16, name="ht45", align_bytes=64)
+                ht = pair["ht"][:, : C * 4]
+            else:
+                ht = keep.tile([P, C * 4], BF16, name=f"ht{e}", align_bytes=64)
+            copy = nc.vector.tensor_copy if e < 3 else nc.scalar.copy
+            copy(
                 ht[:].bitcast(F32).rearrange("p (s u) -> p s u", u=2),
                 turned[e][:, : 2 * C].rearrange("p (u s) -> p s u", u=2),
             )
             ready[e] = ht
 
         def quantise(e):
-            hq = keep.tile([P, C], U32, name=f"hq{e}", align_bytes=64)
-            hs = keep.tile([P, C], U8, name=f"hs{e}", align_bytes=64)
+            hq = keep.tile([P, C], U32, name=f"hq{e}", tag=hq_tag.get(e, f"hq{e}"), align_bytes=64)
+            hs = keep.tile([P, C], U8, name=f"hs{e}", tag=f"hs{e}", align_bytes=64)
             nc.vector.quantize_mx(out=hq[:].bitcast(FP8X4), scales=hs[:], in_=ready[e][:])
             codes[e] = (hq, hs)
 
+        def quantise_pair():
+            hq = keep.tile([P, 2 * C], U32, name="hq45", tag="plain0", align_bytes=64)
+            hs = keep.tile([P, 2 * C], U8, name="hs45", align_bytes=64)
+            nc.vector.quantize_mx(out=hq[:].bitcast(FP8X4), scales=hs[:], in_=pair["ht"][:])
+            codes[4] = (hq[:, :C], hs[:, :C])
+            codes[5] = (hq[:, C:], hs[:, C:])
+
         def second_product(e):
             hq, hs = codes[e]
-            if e < 5:
+            if e in (3, 5):
+                sums[e] = banks[e - 1][:, C : 2 * C]
+            else:
                 banks[e] = bank(SUM_BANK[e])
                 sums[e] = banks[e][:, :C]
-            else:
-                sums[e] = banks[4][:, C : 2 * C]
             nc.tensor.matmul_mx(
                 out=sums[e], lhsT=w2[:, e, :].bitcast(FP4X4), lhsT_scale=w2s[:, e, :],
                 rhs=hq[:].bitcast(FP8X4), rhs_scale=hs[:], start=True, stop=True,
             )
 
-        for lo, hi in ((0, 1), (1, 2), (2, 4), (4, 6)):
-            plain[lo] = keep.tile([P, (hi - lo) * C], F32, name=f"plain{lo}", align_bytes=64)
-
-        def unload(e):
-            lo = min(e, 2)
-            nc.scalar.copy(plain[lo][:, (e - lo) * C : (e - lo + 1) * C], sums[e])
+        def unload(lo, hi):
+            plain[lo] = keep.tile([P, (hi - lo) * C], F32, name=f"plain{lo}", tag="hb3" if lo == 1 else f"plain{lo}", align_bytes=64)
+            nc.scalar.copy(plain[lo][:], banks[lo][:, : (hi - lo) * C])
 
         def scatter_gated(lo, hi):
             nc.vector.tensor_tensor(
                 combined[:].indirect(list_of(lo, hi)), plain[lo][:], gates[:, lo * C : hi * C], MULT
             )
 
-        gather_words(0, 1, "words0")
-        gather_words(1, 2, "words1")
-        for e in range(3):
-            gather_scales(e, e + 1, f"scales{e}")
-        gather_scales(3, 6, "scales3")
-        first_product(0)
-        gather_words(2, 3, "words0")
-        first_product(1)
-        gather_words(3, 6, "words1")
-        first_product(2)
-        gelu(0)
-        turn(0)
-        gelu(1)
-        turn(1)
-        first_product(3)
-        interleave(0)
-        quantise(0)
-        for e in range(1, 5):
-            gelu(e + 1)
-            turn(e + 1)
-            second_product(e - 1)
-            interleave(e)
-            if e + 3 < E:
-                first_product(e + 3)
-            quantise(e)
+        for e in range(2):
+            gather_words(e, e + 1, f"words{e}")
+        for e in range(E):
             if e > 1:
-                unload(e - 2)
-            if e in (2, 3):
-                scatter_gated(e - 2, e - 1)
-        second_product(4)
+                gather_words(e, e + 1, f"words{e}")
+            gather_scales(e, e + 1, f"scales{e}")
+        for e in range(3):
+            first_product(e)
+        gates = keep.tile([P, E * C], F32, name="gates", tag="words0", align_bytes=64)
+        nc.scalar.dma_start(out=gates[:], in_=gate)
+        for e in range(3):
+            gelu(e)
+            turn(e)
+            first_product(e + 3)
+        interleave(0)
+        interleave(1)
+        quantise(0)
+        interleave(2)
+        quantise(1)
+        quantise(2)
+        gelu(3)
+        gelu(4)
+        second_product(0)
+        second_product(1)
+        unload(0, 1)
+        scatter_gated(0, 1)
+        turn(3)
+        turn(4)
+        second_product(2)
+        gelu(5)
+        turn(5)
+        interleave(3)
+        quantise(3)
+        second_product(3)
+        unload(1, 2)
+        scatter_gated(1, 2)
+        interleave(4)
         interleave(5)
-        quantise(5)
-        second_product(5)
-        unload(3)
+        quantise_pair()
+        unload(2, 4)
         scatter_gated(2, 4)
+        second_product(4)
+        second_product(5)
+        unload(4, 6)
+        scatter_gated(4, 6)
 
         pre_gate = []
         for (lo, hi), tag in zip(GATE_COLS, GATE_BANK):
@@ -221,12 +244,10 @@ def tile_moe_ogt_gelu_silu_kernel(
                 out=pre_gate[-1][:, : hi - lo], lhsT=wg[:].bitcast(FP8X4), lhsT_scale=wgs[:],
                 rhs=xw[:, lo:hi].bitcast(FP8X4), rhs_scale=xs[:, lo:hi], start=True, stop=True,
             )
-        opened_a = keep.tile([P, 256], F32, name="opened_a", tag="ht5", align_bytes=64)
-        opened_b = keep.tile([P, 512], F32, name="opened_b", tag="hq5", align_bytes=64)
+        opened_a = keep.tile([P, 256], F32, name="opened_a", tag="plain0", align_bytes=64)
+        opened_b = keep.tile([P, 512], F32, name="opened_b", tag="hs45", align_bytes=64)
         nc.scalar.activation(opened_a[:], pre_gate[0][:, :256], ACT.Silu)
-        nc.scalar.copy(plain[4][:], banks[4][:, : 2 * C])
         nc.scalar.activation(opened_b[:], pre_gate[1][:], ACT.Silu)
-        scatter_gated(4, 6)
 
         result = keep.tile([P, T], F32, name="result", align_bytes=64)
         for (lo, hi), opened in zip(OUT_COLS, (opened_a[:], opened_b[:, :256], opened_b[:, 256:])):

@@ -116,12 +116,21 @@ def tile_moe_ogt_gelu_silu_kernel(
         pre, hidden, turned, ready, sums, plain = {}, {}, {}, {}, {}, {}
         pair = {}
         hb_tag = {5: "hs0"}
-        hq_tag = {0: "hb1", 1: "hb2"}
+        hq_tag = {1: "hb2"}
 
 
         def first_product(e):
             pre[e] = bank(PRE_BANK[e])
             w1 = (w1a, w1b, w1c)[e // 2][:, e % 2, :]
+            if e == 0:
+                pre["first half"] = bank("H")
+                for half, dest in enumerate((pre["first half"], pre[0])):
+                    nc.tensor.matmul_mx(
+                        out=dest[:, :256], lhsT=words[0].bitcast(FP8X4), lhsT_scale=scales[0],
+                        rhs=w1[:, half * 512 : (half + 1) * 512].bitcast(FP4X4),
+                        rhs_scale=w1s[:, 0, half * 256 : (half + 1) * 256], start=True, stop=True,
+                    )
+                return
             nc.tensor.matmul_mx(
                 out=pre[e][:], lhsT=words[e].bitcast(FP8X4), lhsT_scale=scales[e],
                 rhs=w1.bitcast(FP4X4), rhs_scale=w1s[:, e, :], start=True, stop=True,
@@ -129,12 +138,20 @@ def tile_moe_ogt_gelu_silu_kernel(
 
         def gelu(e):
             hb = keep.tile([P, H], BF16, name=f"hb{e}", tag=hb_tag.get(e, f"hb{e}"), align_bytes=64)
+            hidden[e] = hb
+            if e == 0:
+                for half, src in enumerate((pre["first half"], pre[0])):
+                    nc.scalar.activation(
+                        hb[:].rearrange("s (u p d) -> s u p d", u=2, d=2)[:, :, half * 64 : (half + 1) * 64, :],
+                        src[:, :256].rearrange("s (p u d) -> s u p d", u=2, d=2),
+                        ACT.Gelu_apprx_tanh,
+                    )
+                return
             nc.scalar.activation(
                 hb[:].rearrange("s (u p d) -> s u p d", u=2, d=2),
                 pre[e][:].rearrange("s (p u d) -> s u p d", u=2, d=2),
                 ACT.Gelu_apprx_tanh,
             )
-            hidden[e] = hb
 
         def turn(e):
             turned[e] = bank(TURN_BANK[e])
@@ -193,10 +210,14 @@ def tile_moe_ogt_gelu_silu_kernel(
 
         for e in range(2):
             gather_words(e, e + 1, f"words{e}")
-        for e in range(E):
-            if e > 1:
-                gather_words(e, e + 1, f"words{e}")
+        for e in range(2):
             gather_scales(e, e + 1, f"scales{e}")
+        gather_words(2, 3, "words2")
+        gather_scales(2, 3, "scales2")
+        gather_words(3, 4, "words3")
+        gather_scales(3, 4, "scales3")
+        gather_words(4, 5, "words4")
+        gather_scales(4, 6, "scales4")
         for e in range(3):
             first_product(e)
         gates = keep.tile([P, E * C], F32, name="gates", tag="words0", align_bytes=64)
@@ -204,10 +225,13 @@ def tile_moe_ogt_gelu_silu_kernel(
         for e in range(3):
             gelu(e)
             turn(e)
-            first_product(e + 3)
+            if e < 2:
+                first_product(e + 3)
         interleave(0)
-        interleave(1)
+        gather_words(5, 6, "hb0")
         quantise(0)
+        first_product(5)
+        interleave(1)
         interleave(2)
         quantise(1)
         quantise(2)

@@ -18,13 +18,19 @@ MULT = mybir.AluOpType.mult
 ADD = mybir.AluOpType.add
 
 P = 128
+QUADRANT = 32
 LIST_COLS = C // 16
+HALF = H // 2
+SCALE_PERIOD = 14
+
 PRE_BANK = "ABCABC"
+FIRST_HALF_BANK = "H"
 TURN_BANK = "DEFGDE"
-SUM_BANK = "GHFFAA"
+SUM_BANK = {0: "G", 1: "H", 2: "F", 4: "A"}
 GATE_BANK = "BC"
 GATE_COLS = ((0, 256), (256, 768))
 OUT_COLS = ((0, 256), (256, 512), (512, 768))
+VECTOR_COPIES = 3
 
 
 def tile_moe_ogt_gelu_silu_kernel(
@@ -38,222 +44,212 @@ def tile_moe_ogt_gelu_silu_kernel(
         def bank(tag):
             return psum.tile([P, 512], F32, name=tag, tag=tag)
 
-        offsets = keep.tile([P, E * LIST_COLS], U16, name="offsets")
-        xw = keep.tile([P, T], I32, name="xw", align_bytes=64)
-        xs = keep.tile([P, T], U8, name="xs", align_bytes=64)
-        w1s = keep.tile([P, E, H], U8, name="w1s", align_bytes=64)
-        wgs = keep.tile([P, N], U8, name="wgs", align_bytes=64)
-        w1a = keep.tile([P, 2, 2 * H], U8, name="w1a", align_bytes=64)
-        w1b = keep.tile([P, 2, 2 * H], U8, name="w1b", align_bytes=64)
-        w1c = keep.tile([P, 2, 2 * H], U8, name="w1c", align_bytes=64)
-        wg = keep.tile([P, N], I32, name="wg", align_bytes=64)
-        ident = keep.tile([P, P], F32, name="ident", align_bytes=64)
-        warm_out = keep.tile([P, 1], F32, name="warm_out", align_bytes=64)
-        ones = keep.tile([P, 32], F32, name="ones", align_bytes=64)
-        ramp = keep.tile([P, 32], F32, name="ramp", align_bytes=64)
-        lane = keep.tile([P, 32], F32, name="lane", align_bytes=64)
+        def sbuf(shape, dtype, name, takes_over=None):
+            return keep.tile(shape, dtype, name=name, tag=takes_over or name, align_bytes=64)
 
-        def load_plane(plane, rows, queues):
-            for q in range(4):
-                queues[q].dma_start(
-                    out=plane[32 * q : 32 * q + 4].bitcast(I32), in_=rows[4 * q : 4 * q + 4].bitcast(I32)
+        offsets = keep.tile([P, E * LIST_COLS], U16, name="offsets")
+        xw = sbuf([P, T], I32, "xw")
+        xs = sbuf([P, T], U8, "xs")
+        w1s = sbuf([P, E, H], U8, "w1s")
+        wgs = sbuf([P, N], U8, "wgs")
+        w1 = [sbuf([P, 2, 2 * H], U8, f"w1_pair{i}") for i in range(E // 2)]
+        wg = sbuf([P, N], I32, "wg")
+        ident = sbuf([P, P], F32, "ident")
+        warm_out = sbuf([P, 1], F32, "warm_out")
+        ones = sbuf([P, QUADRANT], F32, "ones")
+        ramp = sbuf([P, QUADRANT], F32, "ramp")
+        lane = sbuf([P, QUADRANT], F32, "lane")
+
+        def load_scale_rows(tile, rows, queues):
+            for q, queue in enumerate(queues):
+                queue.dma_start(
+                    out=tile[QUADRANT * q : QUADRANT * q + 4].bitcast(I32), in_=rows[4 * q : 4 * q + 4].bitcast(I32)
                 )
 
-        def load_w1(queue, tile, lo, hi):
-            queue.dma_start(
-                out=tile[:].bitcast(I32), in_=w1_words[lo:hi, 0].rearrange("e p b -> p e b").bitcast(I32)
+        def load_w1_pair(i):
+            nc.sync.dma_start(
+                out=w1[i][:].bitcast(I32), in_=w1_words[2 * i : 2 * i + 2, 0].rearrange("e p b -> p e b").bitcast(I32)
             )
 
-        sync, scalar = nc.sync, nc.scalar
+        both_queues = (nc.scalar, nc.sync, nc.scalar, nc.sync)
         nc.vector.memset(xs[:].bitcast(I32), 0)
         nc.vector.memset(w1s[:].bitcast(I32), 0)
         nc.vector.memset(ones[:], 1.0)
         nc.sync.dma_start(offsets[:], offs)
         nc.sync.dma_start(out=xw[:], in_=x_words[0].rearrange("p t d -> p (t d)").bitcast(I32))
         x_rows = x_scales[0].bitcast(I32)
-        nc.scalar.dma_start(out=xs[98:100].bitcast(I32), in_=x_rows[14:16])
-        nc.scalar.dma_start(out=xs[0:98].bitcast(I32), in_=x_rows[0:14].unsqueeze(0).to_broadcast([7, 14, T // 4]))
-        load_w1(nc.sync, w1a, 0, 2)
-        load_plane(w1s, w1_scales[:, 0].rearrange("e r n -> r e n"), (scalar, sync, scalar, sync))
-        load_w1(nc.sync, w1b, 2, 4)
-        load_w1(nc.sync, w1c, 4, 6)
+        periods = 7
+        covered = periods * SCALE_PERIOD
+        nc.scalar.dma_start(out=xs[covered : covered + 2].bitcast(I32), in_=x_rows[SCALE_PERIOD:16])
+        nc.scalar.dma_start(
+            out=xs[0:covered].bitcast(I32),
+            in_=x_rows[0:SCALE_PERIOD].unsqueeze(0).to_broadcast([periods, SCALE_PERIOD, T // 4]),
+        )
+        load_w1_pair(0)
+        load_scale_rows(w1s, w1_scales[:, 0].rearrange("e r n -> r e n"), both_queues)
+        load_w1_pair(1)
+        load_w1_pair(2)
 
         nc.vector.tensor_tensor_scan(ramp[:], ones[:], ones[:], 0.0, MULT, ADD)
         nc.scalar.activation(warm_out[:], ramp[:, 0:1], ACT.Gelu_apprx_tanh, bias=ones[:, 0:1])
         nc.vector.memset(ident[:], 0.0)
         nc.vector.transpose(lane[:], ramp[:])
-        for q in range(4):
-            part = slice(32 * q, 32 * q + 32)
+        for q in range(P // QUADRANT):
+            part = slice(QUADRANT * q, QUADRANT * (q + 1))
             nc.vector.tensor_tensor(ident[part, part], ramp[part, :], lane[part, :], mybir.AluOpType.is_equal)
 
-        w2s = keep.tile([P, E, N], U8, name="w2s", align_bytes=64)
+        w2s = sbuf([P, E, N], U8, "w2s")
         nc.vector.memset(w2s[:].bitcast(I32), 0)
         nc.vector.memset(wgs[:].bitcast(I32), 0)
-        w2 = keep.tile([P, E, 2 * N], U8, name="w2", align_bytes=64)
-        load_plane(w2s, w2_scales[:, 0].rearrange("e r n -> r e n"), (scalar, sync, scalar, sync))
+        w2 = sbuf([P, E, 2 * N], U8, "w2")
+        load_scale_rows(w2s, w2_scales[:, 0].rearrange("e r n -> r e n"), both_queues)
         nc.sync.dma_start(out=w2[:].bitcast(I32), in_=w2_words[:, 0].rearrange("e p b -> p e b").bitcast(I32))
-        load_plane(wgs, wg_scales[0], (sync,) * 4)
+        load_scale_rows(wgs, wg_scales[0], (nc.sync,) * 4)
         nc.sync.dma_start(out=wg[:], in_=wg_words[0].rearrange("p n d -> p (n d)").bitcast(I32))
 
         def list_of(lo, hi):
             return offsets[:, lo * LIST_COLS : hi * LIST_COLS]
 
-        words, scales, codes, banks = {}, {}, {}, {}
+        words, scales = {}, {}
+        pre, hidden, turned, grouped, codes = {}, {}, {}, {}, {}
+        sums, plain = {}, {}
 
-        def gather_scales(lo, hi, tag):
-            gs = keep.tile([P, (hi - lo) * C], U8, name=f"gs{lo}", tag=tag, align_bytes=64)
-            nc.vector.tensor_copy(gs[:], xs[:].indirect(list_of(lo, hi)))
+        def gather_words(e, takes_over=None):
+            words[e] = sbuf([P, C], U32, f"words{e}", takes_over)
+            nc.vector.tensor_copy(words[e][:], xw[:].bitcast(U32).indirect(list_of(e, e + 1)))
+
+        def gather_scales(lo, hi, takes_over=None):
+            gathered = sbuf([P, (hi - lo) * C], U8, f"scales{lo}", takes_over)
+            nc.vector.tensor_copy(gathered[:], xs[:].indirect(list_of(lo, hi)))
             for e in range(lo, hi):
-                scales[e] = gs[:, (e - lo) * C : (e - lo + 1) * C]
+                scales[e] = gathered[:, (e - lo) * C : (e - lo + 1) * C]
 
-        def gather_words(lo, hi, tag):
-            gw = keep.tile([P, (hi - lo) * C], U32, name=f"gw{lo}", tag=tag, align_bytes=64)
-            nc.vector.tensor_copy(gw[:], xw[:].bitcast(U32).indirect(list_of(lo, hi)))
-            for e in range(lo, hi):
-                words[e] = gw[:, (e - lo) * C : (e - lo + 1) * C]
+        combined = sbuf([P, T], F32, "combined")
 
-        combined = keep.tile([P, T], F32, name="combined", align_bytes=64)
-        pre, hidden, turned, ready, sums, plain = {}, {}, {}, {}, {}, {}
-        pair = {}
-        hb_tag = {5: "hs0"}
-        hq_tag = {1: "hb2"}
-
+        def product_columns(e, dest, lo, hi):
+            nc.tensor.matmul_mx(
+                out=dest, lhsT=words[e][:].bitcast(FP8X4), lhsT_scale=scales[e],
+                rhs=w1[e // 2][:, e % 2, 2 * lo : 2 * hi].bitcast(FP4X4), rhs_scale=w1s[:, e, lo:hi],
+                start=True, stop=True,
+            )
 
         def first_product(e):
-            pre[e] = bank(PRE_BANK[e])
-            w1 = (w1a, w1b, w1c)[e // 2][:, e % 2, :]
+            whole = bank(PRE_BANK[e])
             if e == 0:
-                pre["first half"] = bank("H")
-                for half, dest in enumerate((pre["first half"], pre[0])):
-                    nc.tensor.matmul_mx(
-                        out=dest[:, :256], lhsT=words[0].bitcast(FP8X4), lhsT_scale=scales[0],
-                        rhs=w1[:, half * 512 : (half + 1) * 512].bitcast(FP4X4),
-                        rhs_scale=w1s[:, 0, half * 256 : (half + 1) * 256], start=True, stop=True,
-                    )
-                return
-            nc.tensor.matmul_mx(
-                out=pre[e][:], lhsT=words[e].bitcast(FP8X4), lhsT_scale=scales[e],
-                rhs=w1.bitcast(FP4X4), rhs_scale=w1s[:, e, :], start=True, stop=True,
-            )
+                pre[e] = [(bank(FIRST_HALF_BANK)[:, :HALF], 0), (whole[:, :HALF], HALF)]
+            else:
+                pre[e] = [(whole[:], 0)]
+            for dest, lo in pre[e]:
+                product_columns(e, dest, lo, lo + dest.shape[1])
 
-        def gelu(e):
-            hb = keep.tile([P, H], BF16, name=f"hb{e}", tag=hb_tag.get(e, f"hb{e}"), align_bytes=64)
-            hidden[e] = hb
-            if e == 0:
-                for half, src in enumerate((pre["first half"], pre[0])):
-                    nc.scalar.activation(
-                        hb[:].rearrange("s (u p d) -> s u p d", u=2, d=2)[:, :, half * 64 : (half + 1) * 64, :],
-                        src[:, :256].rearrange("s (p u d) -> s u p d", u=2, d=2),
-                        ACT.Gelu_apprx_tanh,
-                    )
-                return
-            nc.scalar.activation(
-                hb[:].rearrange("s (u p d) -> s u p d", u=2, d=2),
-                pre[e][:].rearrange("s (p u d) -> s u p d", u=2, d=2),
-                ACT.Gelu_apprx_tanh,
-            )
+        def gelu(e, takes_over=None):
+            hidden[e] = sbuf([P, H], BF16, f"hidden{e}", takes_over)
+            by_pair = hidden[e][:].rearrange("s (u p d) -> s u p d", u=2, d=2)
+            for source, lo in pre[e]:
+                nc.scalar.activation(
+                    by_pair[:, :, lo // 4 : (lo + source.shape[1]) // 4, :],
+                    source.rearrange("s (p u d) -> s u p d", u=2, d=2),
+                    ACT.Gelu_apprx_tanh,
+                )
 
         def turn(e):
             turned[e] = bank(TURN_BANK[e])
             pairs = hidden[e][:].bitcast(F32)
-            for half in range(2):
-                nc.tensor.transpose(turned[e][:, half * C : (half + 1) * C], pairs[:, half * P : (half + 1) * P], ident[:])
+            for u in range(2):
+                nc.tensor.transpose(turned[e][:, u * C : (u + 1) * C], pairs[:, u * P : (u + 1) * P], ident[:])
 
-        def interleave(e):
-            if e == 5:
-                ht = pair["ht"][:, C * 4 :]
-            elif e == 4:
-                pair["ht"] = keep.tile([P, C * 8], BF16, name="ht45", align_bytes=64)
-                ht = pair["ht"][:, : C * 4]
-            else:
-                ht = keep.tile([P, C * 4], BF16, name=f"ht{e}", align_bytes=64)
-            copy = nc.vector.tensor_copy if e < 3 else nc.scalar.copy
+        def interleave(e, dest):
+            copy = nc.vector.tensor_copy if e < VECTOR_COPIES else nc.scalar.copy
             copy(
-                ht[:].bitcast(F32).rearrange("p (s u) -> p s u", u=2),
+                dest.bitcast(F32).rearrange("p (s u) -> p s u", u=2),
                 turned[e][:, : 2 * C].rearrange("p (u s) -> p s u", u=2),
             )
-            ready[e] = ht
 
-        def quantise(e):
-            hq = keep.tile([P, C], U32, name=f"hq{e}", tag=hq_tag.get(e, f"hq{e}"), align_bytes=64)
-            hs = keep.tile([P, C], U8, name=f"hs{e}", tag=f"hs{e}", align_bytes=64)
-            nc.vector.quantize_mx(out=hq[:].bitcast(FP8X4), scales=hs[:], in_=ready[e][:])
-            codes[e] = (hq, hs)
+        def interleave_alone(e):
+            grouped[e] = sbuf([P, 4 * C], BF16, f"grouped{e}")
+            interleave(e, grouped[e][:])
 
-        def quantise_pair():
-            hq = keep.tile([P, 2 * C], U32, name="hq45", tag="plain0", align_bytes=64)
-            hs = keep.tile([P, 2 * C], U8, name="hs45", align_bytes=64)
-            nc.vector.quantize_mx(out=hq[:].bitcast(FP8X4), scales=hs[:], in_=pair["ht"][:])
-            codes[4] = (hq[:, :C], hs[:, :C])
-            codes[5] = (hq[:, C:], hs[:, C:])
+        def quantise(lo, hi, takes_over=None):
+            hq = sbuf([P, (hi - lo) * C], U32, f"hq{lo}", takes_over)
+            hs = sbuf([P, (hi - lo) * C], U8, f"hs{lo}")
+            nc.vector.quantize_mx(out=hq[:].bitcast(FP8X4), scales=hs[:], in_=grouped[lo][:])
+            for e in range(lo, hi):
+                cols = slice((e - lo) * C, (e - lo + 1) * C)
+                codes[e] = (hq[:, cols], hs[:, cols])
 
         def second_product(e):
-            hq, hs = codes[e]
-            if e in (3, 5):
-                sums[e] = banks[e - 1][:, C : 2 * C]
+            if e in SUM_BANK:
+                sums[e] = bank(SUM_BANK[e])
+                dest = sums[e][:, :C]
             else:
-                banks[e] = bank(SUM_BANK[e])
-                sums[e] = banks[e][:, :C]
+                dest = sums[e - 1][:, C : 2 * C]
+            hq, hs = codes[e]
             nc.tensor.matmul_mx(
-                out=sums[e], lhsT=w2[:, e, :].bitcast(FP4X4), lhsT_scale=w2s[:, e, :],
-                rhs=hq[:].bitcast(FP8X4), rhs_scale=hs[:], start=True, stop=True,
+                out=dest, lhsT=w2[:, e, :].bitcast(FP4X4), lhsT_scale=w2s[:, e, :],
+                rhs=hq.bitcast(FP8X4), rhs_scale=hs, start=True, stop=True,
             )
 
-        def unload(lo, hi):
-            plain[lo] = keep.tile([P, (hi - lo) * C], F32, name=f"plain{lo}", tag="hb3" if lo == 1 else f"plain{lo}", align_bytes=64)
-            nc.scalar.copy(plain[lo][:], banks[lo][:, : (hi - lo) * C])
+        def unload(lo, hi, takes_over=None):
+            plain[lo] = sbuf([P, (hi - lo) * C], F32, f"plain{lo}", takes_over)
+            nc.scalar.copy(plain[lo][:], sums[lo][:, : (hi - lo) * C])
 
         def scatter_gated(lo, hi):
             nc.vector.tensor_tensor(
                 combined[:].indirect(list_of(lo, hi)), plain[lo][:], gates[:, lo * C : hi * C], MULT
             )
 
-        for e in range(2):
-            gather_words(e, e + 1, f"words{e}")
-        for e in range(2):
-            gather_scales(e, e + 1, f"scales{e}")
-        gather_words(2, 3, "words2")
-        gather_scales(2, 3, "scales2")
-        gather_words(3, 4, "words3")
-        gather_scales(3, 4, "scales3")
-        gather_words(4, 5, "words4")
-        gather_scales(4, 6, "scales4")
+        gather_words(0)
+        gather_words(1)
+        gather_scales(0, 1)
+        gather_scales(1, 2)
+        for e in (2, 3):
+            gather_words(e)
+            gather_scales(e, e + 1)
+        gather_words(4)
+        gather_scales(4, 6)
+
         for e in range(3):
             first_product(e)
-        gates = keep.tile([P, E * C], F32, name="gates", tag="words0", align_bytes=64)
+        gelu(0)
+        turn(0)
+        first_product(3)
+        gates = sbuf([P, E * C], F32, "gates", takes_over="words1")
         nc.scalar.dma_start(out=gates[:], in_=gate)
-        for e in range(3):
-            gelu(e)
-            turn(e)
-            if e < 2:
-                first_product(e + 3)
-        interleave(0)
-        gather_words(5, 6, "hb0")
-        quantise(0)
+        gelu(1)
+        turn(1)
+        first_product(4)
+        gelu(2)
+        turn(2)
+
+        interleave_alone(0)
+        gather_words(5, takes_over="hidden0")
+        quantise(0, 1)
         first_product(5)
-        interleave(1)
-        interleave(2)
-        quantise(1)
-        quantise(2)
+        interleave_alone(1)
+        interleave_alone(2)
+        quantise(1, 2, takes_over="hidden2")
+        quantise(2, 3)
         gelu(3)
         gelu(4)
         second_product(0)
         second_product(1)
         unload(0, 1)
         scatter_gated(0, 1)
+
         turn(3)
         turn(4)
         second_product(2)
-        gelu(5)
+        gelu(5, takes_over="hs0")
         turn(5)
-        interleave(3)
-        quantise(3)
+        interleave_alone(3)
+        quantise(3, 4)
         second_product(3)
-        unload(1, 2)
+        unload(1, 2, takes_over="hidden3")
         scatter_gated(1, 2)
-        interleave(4)
-        interleave(5)
-        quantise_pair()
+        grouped[4] = sbuf([P, 8 * C], BF16, "grouped4")
+        interleave(4, grouped[4][:, : 4 * C])
+        interleave(5, grouped[4][:, 4 * C :])
+        quantise(4, 6, takes_over="plain0")
         unload(2, 4)
         scatter_gated(2, 4)
         second_product(4)
@@ -263,17 +259,17 @@ def tile_moe_ogt_gelu_silu_kernel(
 
         pre_gate = []
         for (lo, hi), tag in zip(GATE_COLS, GATE_BANK):
-            pre_gate.append(bank(tag))
+            pre_gate.append(bank(tag)[:, : hi - lo])
             nc.tensor.matmul_mx(
-                out=pre_gate[-1][:, : hi - lo], lhsT=wg[:].bitcast(FP8X4), lhsT_scale=wgs[:],
+                out=pre_gate[-1], lhsT=wg[:].bitcast(FP8X4), lhsT_scale=wgs[:],
                 rhs=xw[:, lo:hi].bitcast(FP8X4), rhs_scale=xs[:, lo:hi], start=True, stop=True,
             )
-        opened_a = keep.tile([P, 256], F32, name="opened_a", tag="plain0", align_bytes=64)
-        opened_b = keep.tile([P, 512], F32, name="opened_b", tag="hs45", align_bytes=64)
-        nc.scalar.activation(opened_a[:], pre_gate[0][:, :256], ACT.Silu)
-        nc.scalar.activation(opened_b[:], pre_gate[1][:], ACT.Silu)
+        opened_short = sbuf([P, 256], F32, "opened_short", takes_over="plain0")
+        opened_long = sbuf([P, 512], F32, "opened_long", takes_over="hs4")
+        nc.scalar.activation(opened_short[:], pre_gate[0], ACT.Silu)
+        nc.scalar.activation(opened_long[:], pre_gate[1], ACT.Silu)
 
-        result = keep.tile([P, T], F32, name="result", align_bytes=64)
-        for (lo, hi), opened in zip(OUT_COLS, (opened_a[:], opened_b[:, :256], opened_b[:, 256:])):
+        result = sbuf([P, T], F32, "result")
+        for (lo, hi), opened in zip(OUT_COLS, (opened_short[:], opened_long[:, :256], opened_long[:, 256:])):
             nc.vector.tensor_tensor(result[:, lo:hi], combined[:, lo:hi], opened, MULT)
             nc.sync.dma_start(out=out[:, lo:hi], in_=result[:, lo:hi])

@@ -200,11 +200,11 @@ def tile_moe_ogt_gelu_silu_kernel(
 
         gather_words(0)
         gather_words(1)
-        gather_scales(0, 1)
-        gather_scales(1, 2)
-        for e in (2, 3):
-            gather_words(e)
+        gather_words(2)
+        for e in range(3):
             gather_scales(e, e + 1)
+        gather_words(3)
+        gather_scales(3, 4)
         gather_words(4)
         gather_scales(4, 6)
 

@@ -21,13 +21,12 @@ P = 128
 QUADRANT = 32
 LIST_COLS = C // 16
 HALF = H // 2
-SCALE_PERIOD = 14
 
-PRE_BANK = "ABCABC"
+PRE_BANK = "ABCABA"
 FIRST_HALF_BANK = "H"
-TURN_BANK = "DEFGDE"
-SUM_BANK = {0: "G", 1: "H", 2: "F", 4: "A"}
-GATE_BANK = "BC"
+TURN_BANK = "DEFGHG"
+SUM_BANK = {0: "C", 1: "B", 3: "D", 5: "E"}
+GATE_BANK = "AC"
 GATE_COLS = ((0, 256), (256, 768))
 OUT_COLS = ((0, 256), (256, 512), (512, 768))
 VECTOR_COPIES = 3
@@ -50,7 +49,8 @@ def tile_moe_ogt_gelu_silu_kernel(
         offsets = keep.tile([P, E * LIST_COLS], U16, name="offsets")
         xw = sbuf([P, T], I32, "xw")
         xs = sbuf([P, T], U8, "xs")
-        w1s = sbuf([P, E, H], U8, "w1s")
+        w1s_first = sbuf([P, H], U8, "w1s_first")
+        w1s_rest = sbuf([P, E - 1, H], U8, "w1s_rest")
         wgs = sbuf([P, N], U8, "wgs")
         w1 = [sbuf([P, 2, 2 * H], U8, f"w1_pair{i}") for i in range(E // 2)]
         wg = sbuf([P, N], I32, "wg")
@@ -66,27 +66,29 @@ def tile_moe_ogt_gelu_silu_kernel(
                     out=tile[QUADRANT * q : QUADRANT * q + 4].bitcast(I32), in_=rows[4 * q : 4 * q + 4].bitcast(I32)
                 )
 
-        def load_w1_pair(i):
-            nc.sync.dma_start(
+        def load_w1_pair(i, queue=nc.sync):
+            queue.dma_start(
                 out=w1[i][:].bitcast(I32), in_=w1_words[2 * i : 2 * i + 2, 0].rearrange("e p b -> p e b").bitcast(I32)
             )
 
         both_queues = (nc.scalar, nc.sync, nc.scalar, nc.sync)
-        nc.vector.memset(xs[:].bitcast(I32), 0)
-        nc.vector.memset(w1s[:].bitcast(I32), 0)
+        nc.vector.memset(w1s_first[96:128].bitcast(I32), 0)
+        nc.vector.memset(w1s_rest[:].bitcast(I32), 0)
         nc.vector.memset(ones[:], 1.0)
         nc.sync.dma_start(offsets[:], offs)
-        nc.sync.dma_start(out=xw[:], in_=x_words[0].rearrange("p t d -> p (t d)").bitcast(I32))
         x_rows = x_scales[0].bitcast(I32)
-        periods = 7
-        covered = periods * SCALE_PERIOD
-        nc.scalar.dma_start(out=xs[covered : covered + 2].bitcast(I32), in_=x_rows[SCALE_PERIOD:16])
+        for q, queue in enumerate(both_queues):
+            queue.dma_start(
+                out=xs[QUADRANT * q : QUADRANT * (q + 1)].bitcast(I32),
+                in_=x_rows[4 * q : 4 * q + 4].unsqueeze(0).to_broadcast([8, 4, T // 4]),
+            )
+        nc.sync.dma_start(out=xw[:], in_=x_words[0].rearrange("p t d -> p (t d)").bitcast(I32))
+        w1_rows = w1_scales.rearrange("e s r n -> (e s r) n").bitcast(I32)
         nc.scalar.dma_start(
-            out=xs[0:covered].bitcast(I32),
-            in_=x_rows[0:SCALE_PERIOD].unsqueeze(0).to_broadcast([periods, SCALE_PERIOD, T // 4]),
+            out=w1s_first[0:112].bitcast(I32), in_=w1_rows[0:28].unsqueeze(0).to_broadcast([4, 28, H // 4])
         )
-        load_w1_pair(0)
-        load_scale_rows(w1s, w1_scales[:, 0].rearrange("e r n -> r e n"), both_queues)
+        load_w1_pair(0, nc.scalar)
+        load_scale_rows(w1s_rest, w1_scales[1:, 0].rearrange("e r n -> r e n"), both_queues)
         load_w1_pair(1)
         load_w1_pair(2)
 
@@ -129,7 +131,7 @@ def tile_moe_ogt_gelu_silu_kernel(
         def product_columns(e, dest, lo, hi):
             nc.tensor.matmul_mx(
                 out=dest, lhsT=words[e][:].bitcast(FP8X4), lhsT_scale=scales[e],
-                rhs=w1[e // 2][:, e % 2, 2 * lo : 2 * hi].bitcast(FP4X4), rhs_scale=w1s[:, e, lo:hi],
+                rhs=w1[e // 2][:, e % 2, 2 * lo : 2 * hi].bitcast(FP4X4), rhs_scale=(w1s_first[:, lo:hi] if e == 0 else w1s_rest[:, e - 1, lo:hi]),
                 start=True, stop=True,
             )
 
@@ -198,64 +200,59 @@ def tile_moe_ogt_gelu_silu_kernel(
                 combined[:].indirect(list_of(lo, hi)), plain[lo][:], gates[:, lo * C : hi * C], MULT
             )
 
+        for e in range(3):
+            gather_scales(e, e + 1)
         gather_words(0)
         gather_words(1)
         gather_words(2)
-        for e in range(3):
-            gather_scales(e, e + 1)
         gather_words(3)
-        gather_scales(3, 4)
-        gather_words(4)
-        gather_scales(4, 6)
 
         for e in range(3):
             first_product(e)
+        gather_scales(3, 4, takes_over="scales0")
+        gather_words(4)
+        gather_scales(4, 6, takes_over="scales1")
+        gather_words(5)
         gelu(0)
         turn(0)
         first_product(3)
         gates = sbuf([P, E * C], F32, "gates", takes_over="words1")
         nc.scalar.dma_start(out=gates[:], in_=gate)
         gelu(1)
-        turn(1)
         first_product(4)
+        turn(1)
         gelu(2)
         turn(2)
-
         interleave_alone(0)
-        gather_words(5, takes_over="hidden0")
         quantise(0, 1)
-        first_product(5)
         interleave_alone(1)
         interleave_alone(2)
         quantise(1, 2, takes_over="hidden2")
         quantise(2, 3)
-        gelu(3)
-        gelu(4)
         second_product(0)
+        gelu(3)
+        turn(3)
+        first_product(5)
+        gelu(4)
+        turn(4)
         second_product(1)
+        second_product(2)
         unload(0, 1)
         scatter_gated(0, 1)
-
-        turn(3)
-        turn(4)
-        second_product(2)
-        gelu(5, takes_over="hs0")
-        turn(5)
-        interleave_alone(3)
-        quantise(3, 4)
+        grouped[3] = sbuf([P, 8 * C], BF16, "grouped3")
+        interleave(3, grouped[3][:, : 4 * C])
+        interleave(4, grouped[3][:, 4 * C :])
+        quantise(3, 5)
+        unload(1, 3)
+        scatter_gated(1, 3)
         second_product(3)
-        unload(1, 2, takes_over="hidden3")
-        scatter_gated(1, 2)
-        grouped[4] = sbuf([P, 8 * C], BF16, "grouped4")
-        interleave(4, grouped[4][:, : 4 * C])
-        interleave(5, grouped[4][:, 4 * C :])
-        quantise(4, 6, takes_over="plain0")
-        unload(2, 4)
-        scatter_gated(2, 4)
         second_product(4)
-        second_product(5)
-        unload(4, 6)
-        scatter_gated(4, 6)
+        gelu(5, takes_over="hidden4")
+        turn(5)
+        interleave_alone(5)
+        quantise(5, 6)
+        unload(3, 5, takes_over="hidden4")
+        scatter_gated(3, 5)
 
         pre_gate = []
         for (lo, hi), tag in zip(GATE_COLS, GATE_BANK):
@@ -264,9 +261,13 @@ def tile_moe_ogt_gelu_silu_kernel(
                 out=pre_gate[-1], lhsT=wg[:].bitcast(FP8X4), lhsT_scale=wgs[:],
                 rhs=xw[:, lo:hi].bitcast(FP8X4), rhs_scale=xs[:, lo:hi], start=True, stop=True,
             )
-        opened_short = sbuf([P, 256], F32, "opened_short", takes_over="plain0")
-        opened_long = sbuf([P, 512], F32, "opened_long", takes_over="hs4")
-        nc.scalar.activation(opened_short[:], pre_gate[0], ACT.Silu)
+        second_product(5)
+        opened_short = sbuf([P, 256], F32, "opened_short")
+        opened_long = sbuf([P, 512], F32, "opened_long", takes_over="hs5")
+        nc.scalar.activation(opened_short[:, :C], pre_gate[0][:, :C], ACT.Silu)
+        unload(5, 6, takes_over="wg")
+        scatter_gated(5, 6)
+        nc.scalar.activation(opened_short[:, C:], pre_gate[0][:, C:], ACT.Silu)
         nc.scalar.activation(opened_long[:], pre_gate[1], ACT.Silu)
 
         result = sbuf([P, T], F32, "result")

from contextlib import ExitStack

import concourse.mybir as mybir

K, T, E, C, H, N = 512, 768, 6, 128, 512, 128
FLOPS = 2 * K * N * T + 2 * K * H * E * C + 2 * H * N * E * C

F32 = mybir.dt.float32
BF16 = mybir.dt.bfloat16
I32 = mybir.dt.int32
U32 = mybir.dt.uint32
U16 = mybir.dt.uint16
U8 = mybir.dt.uint8
FP8X4 = mybir.dt.float8_e4m3fn_x4
FP4X4 = mybir.dt.float4_e2m1fn_x4
ACT = mybir.ActivationFunctionType
MULT = mybir.AluOpType.mult
ADD = mybir.AluOpType.add

P = 128
QUADRANT = 32
LIST_COLS = C // 16
HALF = H // 2

PRE_BANK = "ABCABA"
FIRST_HALF_BANK = "H"
TURN_BANK = "DEFGHG"
SUM_BANK = {0: "C", 1: "B", 3: "D", 5: "E"}
GATE_BANK = "AC"
GATE_COLS = ((0, 256), (256, 768))
OUT_COLS = ((0, 256), (256, 512), (512, 768))
VECTOR_COPIES = 3


def tile_moe_ogt_gelu_silu_kernel(
    tc, x_words, x_scales, wg_words, wg_scales, w1_words, w1_scales, w2_words, w2_scales, gate, offs, out
):
    nc = tc.nc
    with ExitStack() as ctx:
        keep = ctx.enter_context(tc.tile_pool(name="keep", bufs=1))
        psum = ctx.enter_context(tc.psum_pool(name="psum", bufs=1))

        def bank(tag):
            return psum.tile([P, 512], F32, name=tag, tag=tag)

        def sbuf(shape, dtype, name, takes_over=None):
            return keep.tile(shape, dtype, name=name, tag=takes_over or name, align_bytes=64)

        offsets = keep.tile([P, E * LIST_COLS], U16, name="offsets")
        xw = sbuf([P, T], I32, "xw")
        xs = sbuf([P, T], U8, "xs")
        w1s_first = sbuf([P, H], U8, "w1s_first")
        w1s_rest = sbuf([P, E - 1, H], U8, "w1s_rest")
        wgs = sbuf([P, N], U8, "wgs")
        w1 = [sbuf([P, 2, 2 * H], U8, f"w1_pair{i}") for i in range(E // 2)]
        wg = sbuf([P, N], I32, "wg")
        ident = sbuf([P, P], F32, "ident")
        warm_out = sbuf([P, 1], F32, "warm_out")
        ones = sbuf([P, QUADRANT], F32, "ones")
        ramp = sbuf([P, QUADRANT], F32, "ramp")
        lane = sbuf([P, QUADRANT], F32, "lane")

        def load_scale_rows(tile, rows, queues):
            for q, queue in enumerate(queues):
                queue.dma_start(
                    out=tile[QUADRANT * q : QUADRANT * q + 4].bitcast(I32), in_=rows[4 * q : 4 * q + 4].bitcast(I32)
                )

        def load_w1_pair(i, queue=nc.sync):
            queue.dma_start(
                out=w1[i][:].bitcast(I32), in_=w1_words[2 * i : 2 * i + 2, 0].rearrange("e p b -> p e b").bitcast(I32)
            )

        both_queues = (nc.scalar, nc.sync, nc.scalar, nc.sync)
        nc.vector.memset(w1s_first[96:128].bitcast(I32), 0)
        nc.vector.memset(w1s_rest[:].bitcast(I32), 0)
        nc.vector.memset(ones[:], 1.0)
        nc.sync.dma_start(offsets[:], offs)
        x_rows = x_scales[0].bitcast(I32)
        for q, queue in enumerate(both_queues):
            queue.dma_start(
                out=xs[QUADRANT * q : QUADRANT * (q + 1)].bitcast(I32),
                in_=x_rows[4 * q : 4 * q + 4].unsqueeze(0).to_broadcast([8, 4, T // 4]),
            )
        nc.sync.dma_start(out=xw[:], in_=x_words[0].rearrange("p t d -> p (t d)").bitcast(I32))
        w1_rows = w1_scales.rearrange("e s r n -> (e s r) n").bitcast(I32)
        nc.scalar.dma_start(
            out=w1s_first[0:112].bitcast(I32), in_=w1_rows[0:28].unsqueeze(0).to_broadcast([4, 28, H // 4])
        )
        load_w1_pair(0, nc.scalar)
        load_scale_rows(w1s_rest, w1_scales[1:, 0].rearrange("e r n -> r e n"), both_queues)
        load_w1_pair(1)
        load_w1_pair(2)

        nc.vector.tensor_tensor_scan(ramp[:], ones[:], ones[:], 0.0, MULT, ADD)
        nc.scalar.activation(warm_out[:], ramp[:, 0:1], ACT.Gelu_apprx_tanh, bias=ones[:, 0:1])
        nc.vector.memset(ident[:], 0.0)
        nc.vector.transpose(lane[:], ramp[:])
        for q in range(P // QUADRANT):
            part = slice(QUADRANT * q, QUADRANT * (q + 1))
            nc.vector.tensor_tensor(ident[part, part], ramp[part, :], lane[part, :], mybir.AluOpType.is_equal)

        w2s = sbuf([P, E, N], U8, "w2s")
        nc.vector.memset(w2s[:].bitcast(I32), 0)
        nc.vector.memset(wgs[:].bitcast(I32), 0)
        w2 = sbuf([P, E, 2 * N], U8, "w2")
        load_scale_rows(w2s, w2_scales[:, 0].rearrange("e r n -> r e n"), both_queues)
        nc.sync.dma_start(out=w2[:].bitcast(I32), in_=w2_words[:, 0].rearrange("e p b -> p e b").bitcast(I32))
        load_scale_rows(wgs, wg_scales[0], (nc.sync,) * 4)
        nc.sync.dma_start(out=wg[:], in_=wg_words[0].rearrange("p n d -> p (n d)").bitcast(I32))

        def list_of(lo, hi):
            return offsets[:, lo * LIST_COLS : hi * LIST_COLS]

        words, scales = {}, {}
        pre, hidden, turned, grouped, codes = {}, {}, {}, {}, {}
        sums, plain = {}, {}

        def gather_words(e, takes_over=None):
            words[e] = sbuf([P, C], U32, f"words{e}", takes_over)
            nc.vector.tensor_copy(words[e][:], xw[:].bitcast(U32).indirect(list_of(e, e + 1)))

        def gather_scales(lo, hi, takes_over=None):
            gathered = sbuf([P, (hi - lo) * C], U8, f"scales{lo}", takes_over)
            nc.vector.tensor_copy(gathered[:], xs[:].indirect(list_of(lo, hi)))
            for e in range(lo, hi):
                scales[e] = gathered[:, (e - lo) * C : (e - lo + 1) * C]

        combined = sbuf([P, T], F32, "combined")

        def product_columns(e, dest, lo, hi):
            nc.tensor.matmul_mx(
                out=dest, lhsT=words[e][:].bitcast(FP8X4), lhsT_scale=scales[e],
                rhs=w1[e // 2][:, e % 2, 2 * lo : 2 * hi].bitcast(FP4X4), rhs_scale=(w1s_first[:, lo:hi] if e == 0 else w1s_rest[:, e - 1, lo:hi]),
                start=True, stop=True,
            )

        def first_product(e):
            whole = bank(PRE_BANK[e])
            if e == 0:
                pre[e] = [(bank(FIRST_HALF_BANK)[:, :HALF], 0), (whole[:, :HALF], HALF)]
            else:
                pre[e] = [(whole[:], 0)]
            for dest, lo in pre[e]:
                product_columns(e, dest, lo, lo + dest.shape[1])

        def gelu(e, takes_over=None):
            hidden[e] = sbuf([P, H], BF16, f"hidden{e}", takes_over)
            by_pair = hidden[e][:].rearrange("s (u p d) -> s u p d", u=2, d=2)
            for source, lo in pre[e]:
                nc.scalar.activation(
                    by_pair[:, :, lo // 4 : (lo + source.shape[1]) // 4, :],
                    source.rearrange("s (p u d) -> s u p d", u=2, d=2),
                    ACT.Gelu_apprx_tanh,
                )

        def turn(e):
            turned[e] = bank(TURN_BANK[e])
            pairs = hidden[e][:].bitcast(F32)
            for u in range(2):
                nc.tensor.transpose(turned[e][:, u * C : (u + 1) * C], pairs[:, u * P : (u + 1) * P], ident[:])

        def interleave(e, dest):
            copy = nc.vector.tensor_copy if e < VECTOR_COPIES else nc.scalar.copy
            copy(
                dest.bitcast(F32).rearrange("p (s u) -> p s u", u=2),
                turned[e][:, : 2 * C].rearrange("p (u s) -> p s u", u=2),
            )

        def interleave_alone(e):
            grouped[e] = sbuf([P, 4 * C], BF16, f"grouped{e}")
            interleave(e, grouped[e][:])

        def quantise(lo, hi, takes_over=None):
            hq = sbuf([P, (hi - lo) * C], U32, f"hq{lo}", takes_over)
            hs = sbuf([P, (hi - lo) * C], U8, f"hs{lo}")
            nc.vector.quantize_mx(out=hq[:].bitcast(FP8X4), scales=hs[:], in_=grouped[lo][:])
            for e in range(lo, hi):
                cols = slice((e - lo) * C, (e - lo + 1) * C)
                codes[e] = (hq[:, cols], hs[:, cols])

        def second_product(e):
            if e in SUM_BANK:
                sums[e] = bank(SUM_BANK[e])
                dest = sums[e][:, :C]
            else:
                dest = sums[e - 1][:, C : 2 * C]
            hq, hs = codes[e]
            nc.tensor.matmul_mx(
                out=dest, lhsT=w2[:, e, :].bitcast(FP4X4), lhsT_scale=w2s[:, e, :],
                rhs=hq.bitcast(FP8X4), rhs_scale=hs, start=True, stop=True,
            )

        def unload(lo, hi, takes_over=None):
            plain[lo] = sbuf([P, (hi - lo) * C], F32, f"plain{lo}", takes_over)
            nc.scalar.copy(plain[lo][:], sums[lo][:, : (hi - lo) * C])

        def scatter_gated(lo, hi):
            nc.vector.tensor_tensor(
                combined[:].indirect(list_of(lo, hi)), plain[lo][:], gates[:, lo * C : hi * C], MULT
            )

        for e in range(3):
            gather_scales(e, e + 1)
        gather_words(0)
        gather_words(1)
        gather_words(2)
        gather_words(3)

        for e in range(3):
            first_product(e)
        gather_scales(3, 4, takes_over="scales0")
        gather_words(4)
        gather_scales(4, 6, takes_over="scales1")
        gather_words(5)
        gelu(0)
        turn(0)
        first_product(3)
        gates = sbuf([P, E * C], F32, "gates", takes_over="words1")
        nc.scalar.dma_start(out=gates[:], in_=gate)
        gelu(1)
        first_product(4)
        turn(1)
        gelu(2)
        turn(2)
        interleave_alone(0)
        quantise(0, 1)
        interleave_alone(1)
        interleave_alone(2)
        quantise(1, 2, takes_over="hidden2")
        quantise(2, 3)
        second_product(0)
        gelu(3)
        turn(3)
        first_product(5)
        gelu(4)
        turn(4)
        second_product(1)
        second_product(2)
        unload(0, 1)
        scatter_gated(0, 1)
        grouped[3] = sbuf([P, 8 * C], BF16, "grouped3")
        interleave(3, grouped[3][:, : 4 * C])
        interleave(4, grouped[3][:, 4 * C :])
        quantise(3, 5)
        unload(1, 3)
        scatter_gated(1, 3)
        second_product(3)
        second_product(4)
        gelu(5, takes_over="hidden4")
        turn(5)
        interleave_alone(5)
        quantise(5, 6)
        unload(3, 5, takes_over="hidden4")
        scatter_gated(3, 5)

        pre_gate = []
        for (lo, hi), tag in zip(GATE_COLS, GATE_BANK):
            pre_gate.append(bank(tag)[:, : hi - lo])
            nc.tensor.matmul_mx(
                out=pre_gate[-1], lhsT=wg[:].bitcast(FP8X4), lhsT_scale=wgs[:],
                rhs=xw[:, lo:hi].bitcast(FP8X4), rhs_scale=xs[:, lo:hi], start=True, stop=True,
            )
        second_product(5)
        opened_short = sbuf([P, 256], F32, "opened_short")
        opened_long = sbuf([P, 512], F32, "opened_long", takes_over="hs5")
        nc.scalar.activation(opened_short[:, :C], pre_gate[0][:, :C], ACT.Silu)
        unload(5, 6, takes_over="wg")
        scatter_gated(5, 6)
        nc.scalar.activation(opened_short[:, C:], pre_gate[0][:, C:], ACT.Silu)
        nc.scalar.activation(opened_long[:], pre_gate[1], ACT.Silu)

        result = sbuf([P, T], F32, "result")
        for (lo, hi), opened in zip(OUT_COLS, (opened_short[:], opened_long[:, :256], opened_long[:, 256:])):
            nc.vector.tensor_tensor(result[:, lo:hi], combined[:, lo:hi], opened, MULT)
            nc.sync.dma_start(out=out[:, lo:hi], in_=result[:, lo:hi])
